import numpy as np, ml_dtypes
CORES = [16,18,20,22]
N = 4
BF = ml_dtypes.bfloat16
W, L, C, SX, SL, STEPS = 4096, 1024, 256, 16, 4, 4
def node(q, w):
    u = np.add.reduce(w[..., None] * q, axis=2) & (W - 1)
    return ((u * u >> 5) + 37 * u) & (W - 1)
def parts(rng):
    X = rng.integers(0, 256, (N, 8, 16, W))
    G = np.repeat(rng.integers(0, W, (1, 8, 16, L)), N, axis=0); cut = rng.integers(0, 22, (N, 8, 1, L))
    G = np.where((np.arange(16)[:, None] >= cut) | (rng.random(G.shape) < 0.05), rng.integers(0, W, G.shape), G)
    D = np.repeat(rng.integers(0, L, (1, 8, W)), N, axis=0); D = np.where(rng.random(D.shape) < 0.3, rng.integers(0, L, D.shape), D)
    q = rng.integers(0, 256, (N, 8, 16, C)); E = rng.integers(0, W, (N, 8, 16, C)); w = rng.integers(0, 256, (N, 8, 16))
    th = np.stack([rng.choice(np.array([500, 1100, 1300, 1450, 1600]), (N, 8)) + rng.integers(0, 60, (N, 8)), rng.integers(1000, 1650, (N, 8))], axis=2)
    return X, G, D, q, E, w, th
def pack(X, G, D, q, E, w, th):
    return {"xr": X.reshape(N, 128, W).astype(np.float32).astype(BF), "lg": G.reshape(N, 128, L).astype(np.int32), "dr": D.astype(np.int32), "qd": q.reshape(N, 128, C).astype(np.float32).astype(BF),
            "e0": E.reshape(N, 128, C).astype(np.int32), "wt": w.reshape(N, 128, 1).astype(np.float32).astype(BF), "th": th.astype(np.int32)}
def setup_inputs(rng):
    return pack(*parts(rng))
def setup_inputs_spread(rng):
    X, G, D, q, E, w, th = parts(rng)
    X = np.minimum((np.exp2(8 * rng.random((N, 8, 1, W))) * (0.25 + rng.random(X.shape))).astype(np.int64), 255)
    q = np.minimum((np.exp2(8 * rng.random((N, 8, 1, C))) * (0.25 + rng.random(q.shape))).astype(np.int64), 255)
    w = np.minimum(np.exp2(8 * rng.random(w.shape)).astype(np.int64), 255); th = np.minimum(np.exp2(5 + 7 * rng.random(th.shape)).astype(np.int64), 4079)
    G = np.where(rng.random(G.shape) < 0.5, G, (W * rng.random(G.shape) ** 3).astype(np.int64)); D = np.where(rng.random(D.shape) < 0.5, D, (L * rng.random(D.shape) ** 3).astype(np.int64))
    E = (W * rng.random(E.shape) ** 2).astype(np.int64)
    return pack(X, G, D, q, E, w, th)
def ends_of(rng, shape, hi, share):
    return np.where(rng.random(shape) < share, hi * rng.integers(0, 2, shape), rng.integers(0, hi + 1, shape))
def setup_inputs_ends(rng):
    kx, kq = rng.random((N, 8, 1, W)), rng.random((N, 8, 1, C))
    X = np.where(kx < 0.2, 0, np.where(kx < 0.4, 255, 255 * rng.integers(0, 2, (N, 8, 16, W)))); q = np.where(kq < 0.2, 0, np.where(kq < 0.4, 255, 255 * rng.integers(0, 2, (N, 8, 16, C))))
    X[:, ::2, :, 0] = 255; X[:, ::2, :, W - 1] = 0; X[:, 1::2, :, 0] = 0; X[:, 1::2, :, W - 1] = 255
    G = ends_of(rng, (N, 8, 16, L), W - 1, 0.7); D = ends_of(rng, (N, 8, W), L - 1, 0.7); E = ends_of(rng, (N, 8, 16, C), W - 1, 0.7)
    free = np.argsort(rng.random((N, 8, 16)), axis=2) < 4
    w = np.where(free, rng.integers(0, 256, (N, 8, 16)), 255 * rng.integers(0, 2, (N, 8, 16))); w[:, 0, 0] = 0; w[:, 0, 1] = 255; w[N - 1, 7] = 255
    r, g = np.arange(N)[:, None], np.arange(8)[None, :]
    th = np.stack([np.where((r + g) % 2 == 0, 4079, 0), np.where((g % 2 == 1) & (g < 7), rng.integers(1000, 3000, (N, 8)), np.where((r + (g >> 1)) % 2 == 0, 0, 4079))], axis=2); th[N - 1, 7] = 4079
    q[:, 7, :, C - 1] = 255; q[:, 6, :, C - 1] = 0; q[N - 1, 7][:, [0, 1, C - 1]] = 255
    n = node(q, w)
    for a in range(N):
        D[a, 7, n[a, 7, C - 1]] = L - 1; D[(a + 1) % N, 7, n[a, 7, C - 1]] = L - 1
        G[a, 7, :, L - 1] = (W - 1) * ((a + 1) % 2)
    G[N - 1, 7, :, L - 1] = 0; G[0, 7, :, L - 1] = W - 1; G[0, 7, 15, L - 1] = 0
    return pack(X, G, D, q, E, w, th)
def setup_inputs_corners(rng):
    X, G, D, q, E, w, th = parts(rng)
    m = rng.integers(3, 30, (N, 8)); th[:, :, 0] = 32 * m - 1; th[:, :, 1] = 16 * m; m = m[:, :, None, None]; one = np.eye(16, dtype=np.int64)
    w[..., 0] = 0; w[..., 15] = 255
    nm = SX * np.argsort(rng.random((8, C)), axis=1)[:, :, None] + np.arange(5)
    r0 = rng.integers(4, 90, (N, 8, C, 16)); r2 = r0 + 2 * m
    rec = np.stack([r0, r2 - one[0], r2, r0 - one[1] - one[2], r2 + one[1] + one[2]], axis=3)
    kd = rng.choice(np.array([0, 1, 8, 14, 15, 16]), (N, 8, C)); ks = np.minimum(kd, 15); side = rng.integers(-1, 2, (N, 8, C))
    d = r0 + m + side[..., None] * one[0]
    q = np.ascontiguousarray((d + np.where(kd[..., None] == 0, 0, r0)).transpose(0, 1, 3, 2))
    st = np.maximum(ks + 1, rng.choice(np.array([0, 5, 15, 16]), (N, 8, C)))[..., None]; kk = np.arange(16)
    hj = np.where(kk < st, 0, 3); fj = np.where(kk < kd[..., None], rng.integers(0, 2, (N, 8, C, 16)), np.where(kk < st, 2, 4))
    pal = np.broadcast_to(nm, (N, 8, C, 5)); hn = np.take_along_axis(pal, hj, 3); fn = np.take_along_axis(pal, fj, 3)
    n = node(q, w); col = SL * np.arange(C)
    for a in range(N):
        b = (a + 1) % N
        for g in range(8):
            X[a, g][:, nm[g].reshape(-1)] = rec[a, g].reshape(-1, 16).T
            G[a, g][:, col] = hn[a, g].T; G[b, g][:, col + 1] = fn[a, g].T
            D[b, g, n[a, g]] = col + 1
    for a in range(N):
        for g in range(8): D[a, g, n[a, g]] = col
    return pack(X, G, D, q, E, w, th)
def setup_inputs_crowd(rng):
    X, G, D, q, E, w, th = parts(rng)
    q[:3] = rng.integers(200, 256, q[:3].shape); w[:, 1:3, 0] = 1; w[:, 6] = 0
    q[:, 0:3] = q[:, 0:3, :, :1].copy(); q[:, 1, 0, C - 1] ^= 1; q[:, 2, 0, 0] ^= 1
    q[:, 3, :, 0::2] = q[:, 3, :, :1].copy(); q[:, 3, :, 1::2] = q[:, 3, :, 1:2].copy()
    D[:, 4] = rng.choice(np.array([0, L - 1, L // 2]), (N, W)); G[:, 5, 1:] = rng.choice(np.array([0, 1, W - 1]), (N, 15, L))
    nm = 2 * rng.permutation(W >> 1)[:N] + 1
    for a in range(N): G[a, :, 0, :] = nm[a]
    for a in range(2): X[a, :, :, nm[a]] = 0; X[a, :, :, nm[a + 1]] = 255; th[a, :, 0] = 0
    X[2, :, :, nm[2]] = 255; X[2, :, :, nm[3]] = 0; th[2, :, 0] = 0
    q[1, 7, :, C - 1] = 0
    v = np.arange(1, 4081); u = (255 * v) & (W - 1); k = W - 1 - (((u * u >> 5) + 37 * u) & (W - 1))
    j = int(rng.choice(np.flatnonzero((k >= 1) & (k <= 7 * (C - 1))))); v, u, k = int(v[j]), int(u[j]), int(k[j])
    X[3][:, :, nm] = 0; X[3][:, :, nm[3]] = 255; th[3] = 0; G[3, :, 1, :] = nm[2]
    w[3] = 0; w[3, 7] = rng.permutation(v // 16 + (np.arange(16) < v % 16))
    lose = rng.permutation(7 * (C - 1))[:k]; q[3] = 255; q[3, lose // (C - 1), :, 1 + lose % (C - 1)] = 0
    D[3, :7] |= 1; D[3, 7, W - 1] = SL * int(rng.integers(0, C)) + ((u & (SL - 1)) ^ 1); E[3, 7, :, 0] = nm[3]
    return pack(X, G, D, q, E, w, th)
def setup_inputs_brink(rng):
    X, G, D, q, E, w, th = parts(rng); nm = rng.permutation(W)[:6]
    for a in range(N):
        b = a % 2; own, oth = nm[b], nm[1 - b]
        for g in (0, 7):
            G[a, g, 0, :] = own; X[a, g, :, own] = 0; X[a, g, :, oth] = 0; X[a, g, int(rng.integers(0, 16)), oth] = 1
            q[a, g, :, 1::2] = 255; th[a, g, 0] = 0
        G[a, 2, 0, :] = own; G[a, 2, 3, :] = nm[2 + b]; X[a, 2, :, own] = 0; X[a, 2, :, oth] = 255; X[a, 2, int(rng.integers(0, 16)), oth] = 254
        X[a, 2, :, nm[2 + b]] = 255; X[a, 2, :, nm[3 - b]] = 0; th[a, 2, 0] = 4079
        G[a, 4, 0, :] = own; G[a, 4, 1, :] = nm[4]; G[a, 4, 2, :] = nm[5]; X[a, 4, :, own] = 200; X[a, 4, :, oth] = 100
        X[a, 4, :, nm[4]] = 0; X[a, 4, int(rng.integers(0, 16)), nm[4]] = 1; X[a, 4, :, nm[5]] = 0
        q[a, 4, :, 1::2] = 255; th[a, 4, 0] = 0; th[a, 4, 1] = 4079
    for v in (X, G, D, q, E, w, th): v[2] = v[0]; v[3] = v[1]
    return pack(X, G, D, q, E, w, th)
def check_inputs(d):
    bad = []
    for k, hi in (("xr", 255), ("lg", W - 1), ("dr", L - 1), ("qd", 255), ("e0", W - 1), ("wt", 255), ("th", 4079)):
        v = np.asarray(d[k]).astype(np.float64)
        if not (np.min(v) >= 0 and np.max(v) <= hi): bad.append("range of " + k)
        elif np.any(v != np.floor(v)): bad.append("whole numbers of " + k)
    return bad
def column(logs, book, n):
    return np.take_along_axis(logs, np.take_along_axis(book, n, 1)[:, None, :], 2)
def records(X, names):
    return np.take_along_axis(X, np.ascontiguousarray(names.transpose(0, 2, 1)).reshape(8, 1, C * 16), 2).reshape(8, 16, C, 16)
def reference(xr, lg, dr, qd, e0, wt, th):
    X = xr.astype(np.float32).astype(np.int32).reshape(N, 8, 16, W); G = lg.astype(np.int32).reshape(N, 8, 16, L); D = dr.astype(np.int64).reshape(N, 8, W)
    q = qd.astype(np.float32).astype(np.int32).reshape(N, 8, 16, C); E = e0.astype(np.int32).reshape(N, 8, 16, C)
    w = wt.astype(np.float32).astype(np.int32).reshape(N, 8, 16, 1); h = th.astype(np.int64).reshape(N, 8, 2); A = np.zeros(N, np.int64)
    kk = np.arange(16); i = np.arange(C)
    for t in range(STEPS):
        u = np.add.reduce(w * q, axis=2).astype(np.int64) & (W - 1)
        n = ((u * u >> 5) + 37 * u + A[:, None, None]) & (W - 1)
        own, other = [], []
        for r in range(N):
            f = (r + 1 + t % (N - 1)) % N
            own.append(column(G[r], D[r], n[r])); other.append(column(G[f], D[f], n[r]))
        for r in range(N):
            P, B = own[r], other[r]
            x = records(X[r], P); y = records(X[r], B)
            apart = np.add.reduce(np.abs(x - y), axis=1) > h[r, :, 0][:, None, None]
            ks = np.where(np.any(apart, axis=2), np.argmax(apart, axis=2), 15)
            M = np.max(np.where(kk < ks[:, None, :, None], x, 0), axis=3)
            d = np.abs(q[r] - M)
            xs = np.take_along_axis(x, ks[:, None, :, None], 3)[..., 0]; ys = np.take_along_axis(y, ks[:, None, :, None], 3)[..., 0]
            lost = np.add.reduce(np.abs(ys - d), axis=1) < np.add.reduce(np.abs(xs - d), axis=1)
            z = np.where(lost[:, None, :, None], y, x)
            over = (np.add.reduce(np.abs(z - d[..., None]), axis=1) > h[r, :, 1][:, None, None]) & (kk > ks[:, :, None])
            e = np.where(np.any(over, axis=2), np.argmax(over, axis=2), 16)
            last = np.take_along_axis(z, (e - 1)[:, None, :, None], 3)[..., 0]
            E[r] = np.where(kk[None, :, None] < e[:, None, :], np.where((kk[None, :, None] >= ks[:, None, :]) & lost[:, None, :], B, P), E[r])
            cl = SL * i + (u[r] & (SL - 1)); cx = (SX * i + (u[r] & (SX - 1)))[:, None, :]
            np.put_along_axis(G[r], cl[:, None, :], E[r], 2)
            old = np.take_along_axis(X[r], cx, 2); np.put_along_axis(X[r], cx, (old + d) >> 1, 2)
            if t + 1 < STEPS:
                for g in range(8):
                    v, first = np.unique(n[r, g], return_index=True)
                    D[r, g, v] = cl[g, first]
            q[r] = (d + last) >> 1; A[r] = np.count_nonzero(lost)
    return {"yl": G.reshape(N, 128, L).astype(np.float32), "yx": X.reshape(N, 128, W).astype(np.float32).astype(BF), "yq": q.reshape(N, 128, C).astype(np.float32).astype(BF)}

@@ -1,0 +1,476 @@
+from concourse.mybir import AluOpType as O, ActivationFunctionType as AF
+
+NC, CH, BL, STEPS = 256, 64, 128, 4
+NB, BW_ = NC // BL, BL // 16
+WB = BL * 16 + 32
+f32, bf, i32, u16, f16 = "float32", "bfloat16", "int32", "uint16", "float16"
+SCRATCH = {}
+for _dt, _names in ((bf, "X:4096 XG:%d DF:%d PM:%d AD:4096 AX:4096 ZG:4096 d:256 SM:%d QB:256 Q2:256 W1:1 ON:256 G8:24 F:144 F0:144 FE:144 "
+                     "WF:144 BDa:128 BD:128 NBD:128 ID:128 NI:128 I8:128 N8:128 HI:128 QI:128 HN:128 TI:128 TS:128 R15:128 ETb:2048 BW0:8 OLD:256 NX:256 "
+                     "CB:256 S1:256 AL:512 MG:256 XS:256 DS:256 XL:256 AB:512 ML:256 S2:256 A2:256 JK:128" % (NB * WB, NB * WB, NB * WB, BL * 16)),
+                    (f32, "L:1024 E:256 COL:16 IO:16 CI:64 B32:64 T37:16 CF:32 NW:16 CV:256 FL:16 DO:16 ZD:256 ZN:256 EZ:256 EM:256 AC:1"),
+                    (i32, "D:4352 LI:1024 EI:256 TH:2 PI:2 UI:16 U:16 US:16 SH:16 NN:16 N:16 LO:32"),
+                    (u16, "ZU:256 NU:64 RQ:64 RP:1024 BU:1024 LU:16 LS:16 PU:256 CU:32 DU:16 OF:16 OE:16"),
+                    (f16, "F0h:144 ET:2048 LG:256 SG:256 NH:32 NR:256 PH:256 BH:256 K2:128 IDh:128 NIh:128")):
+    for _x in _names.split():
+        SCRATCH[_x.split(":")[0]] = ("sbuf", [128, int(_x.split(":")[1])], _dt)
+SCRATCH["EQ"] = ("sbuf", [128, 16, 256], bf)
+SCRATCH["TRIM"] = ("sbuf", [128, 16, 16], bf)
+for _p in ("psU", "psW", "psE", "psB0", "psB1", "psZ0", "psZ1", "psZ2"):
+    SCRATCH[_p] = ("psum", [128, 512], f32)
+SEMAPHORES = ["cv", "cs", "ct", "cg", "ls"] + ["dma%d" % k for k in range(16)] + ["%s%d" % (x, k) for x in ("rq", "bu") for k in range(STEPS)]
+
+CY, PEC, GA, SC, FX, WAKE, HOP, RISS = 0.00095, 0.0005, 1.5, 3.5, 0.065, 0.06, 1.6, 0.5
+G3V = ((1, 0), (1, 0))
+TWEAKS = ((44348, 0.7), (22955, 0.7), (83941, 1.5), (59513, 0.7), (97583, 0.3), (82455, 0.3), (77474, 0.3), (72586, 0.3), (51897, 0.3),
+          (99409, 1.5), (6188, 0.7), (51193, 0.3), (58577, 0.7), (57939, 0.3), (27328, 1.5), (8204, 0.3), (37839, 0.3))
+STAG, SEED, NOISE, ROUNDS, LOOK = 0.5, 295390, 2, 12, 0.05
+
+
+def program(g, core, T, topo):
+    rank, ops, acc = T.rank_of(core), [], {}
+    nsem, bias = [0], [0.0]
+
+    def c(name, lo=0, hi=None, st=1):
+        hi = SCRATCH[name][1][-1] if hi is None else hi
+        return [(T[name][:, lo:hi:st] if st > 1 else T[name][:, lo:hi], name, lo, hi, st == 1, (hi - lo + st - 1) // st)]
+
+    def raw(ap, name, lo, hi, full=False):
+        return [(ap, name, lo, hi, full, hi - lo)]
+
+    def ind(win, off):
+        return [(win[0][0].indirect(off[0][0]),) + win[0][1:5] + (16 * off[0][5],)] + off
+
+    def add(q, dur, outs, ins, call, sem=None, n=1, deps=(), lat=0.0, after=()):
+        me, hard, soft = len(ops), set(deps), set(after)
+        ops.append({"q": q, "sem": sem})
+        both = [(False, x) for x in ins if x[1] is not None] + [(True, x) for x in outs if x[1] is not None]
+        for is_w, (_, name, lo, hi, full, _n) in both:
+            if name[:2] == "ps":
+                e = acc.setdefault(name, [q, [], []])
+                if e[0] != q:
+                    e[0], e[1], e[2] = q, [], e[1]
+                hard.update(e[2])
+                e[1].append(me)
+                continue
+            for (l2, h2, w2, o) in acc.get(name, ()):
+                if o != me and l2 < hi and lo < h2 and (is_w or w2):
+                    hard.add(o)
+        for is_w, (_, name, lo, hi, full, _n) in both:
+            if name[:2] != "ps":
+                old = acc.get(name, [])
+                if is_w and full:
+                    old = [a for a in old if not (lo <= a[0] and a[1] <= hi)]
+                acc[name] = old + [(lo, hi, is_w, me)]
+        soft -= hard
+        ops[me] = {"q": q, "dur": dur, "hard": sorted(hard), "soft": sorted(soft), "call": call, "sem": sem, "n": n, "lat": lat, "bias": bias[0]}
+        return me
+
+    def cost(out, a, k):
+        if len(out) > 1:
+            return FX + a[0][5] * SC * CY
+        if a is not None and len(a) > 1:
+            return FX + a[0][5] * GA * CY
+        return FX + max(64, out[0][5] * k) * CY
+
+    def vcopy(out, a, k=1.0):
+        return add("v", cost(out, a, k), out[:1], a + out[1:], lambda: g.vector.tensor_copy(out=out[0][0], in_=a[0][0]))
+
+    def vtt(out, a, b, op):
+        ps = a[0][1][:2] == "ps" or b[0][1][:2] == "ps"
+        return add("v", cost(out, a, 1.0 if ps else 2.0), out, a + b,
+                   lambda: g.vector.tensor_tensor(out=out[0][0], in0=a[0][0], in1=b[0][0], op=op))
+
+    def vts(out, a, s1, s2, o0, o1=None, k=1.0):
+        ex = [x for s in (s1, s2) if isinstance(s, list) for x in s]
+        v1, v2 = [s[0][0] if isinstance(s, list) else s for s in (s1, s2)]
+        kw = {"op0": o0} if o1 is None else {"op0": o0, "op1": o1}
+        return add("v", cost(out, a, k), out, a + ex,
+                   lambda: g.vector.tensor_scalar(out=out[0][0], in0=a[0][0], scalar1=v1, scalar2=v2, **kw))
+
+    def vset(out, v, k=1.0):
+        return add("v", cost(out, None, k), out, [], lambda: g.vector.memset(out[0][0], v))
+
+    def act(out, a, fn, bias=None, scale=None, accum=None):
+        kw = {}
+        if bias is not None:
+            kw["bias"] = bias[0][0] if isinstance(bias, list) else bias
+        if scale is not None:
+            kw["scale"] = scale[0][0] if isinstance(scale, list) else scale
+        if accum is not None:
+            kw["accum_out"] = accum[0][0]
+        return add("s", cost(out, a, 1.0) + 0.02, out + (accum or []), a + [x for s in (bias, scale) if isinstance(s, list) for x in s],
+                   lambda: g.scalar.activation(out=out[0][0], in_=a[0][0], func=fn, **kw))
+
+    def mm(lst, after=()):
+        def call():
+            x = None
+            for (o, l, r, s, e) in lst:
+                x = g.tensor.matmul(out=o[0][0], lhsT=l[0][0], rhs=r[0][0], start=s, stop=e)
+            return x
+        return add("t", 0.08 + sum(max(64, x[2][0][5]) for x in lst) * PEC, [lst[0][0][0]], [v for x in lst for v in x[1] + x[2]], call, after=after)
+
+    def dma(q, out, a, us, calls=None):
+        s = "dma%d" % nsem[0]
+        nsem[0] += 1
+        lst = calls or [(out[0][0], a[0][0])]
+
+        def call():
+            for (o, i) in lst:
+                {"y": g.sync, "s": g.scalar}[q].dma_start(o, i).then_inc(T.sem[s], 16)
+        return add(q, 0.1 * len(lst), out, a, call, sem=s, n=16 * len(lst), lat=us)
+
+    def send(to, src, dst, sem):
+        to = T.cores[to]
+        if not topo.may_write(core, to):
+            raise ValueError("this core may not write to core %d" % to)
+        eng = topo.engines(core, to)[::2]
+        mask = sum(1 << e for e in eng)
+        rid, pid = topo.addr(to)[:2]
+
+        def call():
+            g.remote_dma(dst[0][0], src[0][0], T.sem[sem], T.sem["ls"], pid, rid, mask)
+        o = add("g", RISS, [], src, call, sem="ls", n=len(eng))
+        add("r" + sem, 0.0, dst, [], None, sem=sem, n=len(eng), deps=(o,), lat=HOP)
+        return o
+
+    def dram(ap):
+        return [(ap, None, 0, 0, False, 0)]
+
+    def asel(out, a, pat, op, base, cm, deps=()):
+        return add("g", 0.2 + out[0][5] * 2 * CY, out, a, lambda: g.affine_select(
+            out=out[0][0], in_=a[0][0], pattern=pat, compare_op=op, fill=0.0, base=base, channel_multiplier=cm), deps=deps)
+
+    def iota(out, pat, base, cm):
+        return add("g", 0.15 + out[0][5] * 2 * CY, out, [], lambda: g.iota(
+            out[0][0], pat, base, cm, allow_small_or_imprecise_dtypes=True))
+
+    bias[0] = 100.0
+    dma("y", c("QB"), dram(T.qd[:, :]), 2.0)
+    dma("s", c("W1"), dram(T.wt[:]), 2.0)
+    bias[0] = 200.0
+    vset(c("ON"), 1.0, 0.5)
+    vset(c("F"), 0.0, 0.5)
+    vset(c("F0"), 0.0, 0.5)
+    cut = 3072
+    asel(c("G8", 0, 8), c("ON", 0, 8), [[-16, 8]], O.is_ge, 0, 1)
+    asel(c("G8", 8, 16), c("G8", 0, 8), [[16, 8]], O.is_ge, 15, -1)
+    asel(c("G8", 16, 24), c("ON", 0, 8), [[-16, 8]], O.is_equal, 0, 1)
+    bias[0] = 100.0
+    vset(c("D", 0, cut), 0.0)
+    iota(c("D", cut, 4352), [[0, 4352 - cut]], 0, 0)
+    dma("y", raw(T.D[0:128:16, 0:4096], "D", 0, 4096), dram(T.dr[:, :]), 2.5)
+    vcopy(c("F", 16, 144, 16), c("G8", 8, 16))
+    vcopy(c("F0", 16, 144, 16), c("G8", 16, 24))
+    vts(c("WF"), c("F"), c("W1"), 0.5, O.mult, O.mult)
+    vcopy(c("F0h"), c("F0"))
+    act(c("Q2"), c("QB"), AF.Copy, scale=2.0)
+    bias[0] = 0.0
+    dma("s", c("LI"), dram(T.lg[:, :]), 3.0)
+    for k in range(2):
+        dma("ys"[k], c("X", 2048 * k, 2048 * k + 2048), dram(T.xr[:, 2048 * k:2048 * k + 2048]), 4.0)
+    dma("s", c("EI"), dram(T.e0[:, :]), 4.0)
+    dma("y", raw(T.TH[:, :], "TH", 0, 2, True), dram(None), 4.0, [(T.TH[j:128:16, :], T.th[:, :]) for j in range(16)])
+    iota(c("PI", 0, 1), [[0, 1]], 0, 1)
+    iota(c("CI", 0, 16), [[256, 16]], 0, 0)
+    iota(c("CI", 16, 32), [[0, NB], [64, BW_]], 0, 0)
+    iota(c("CI", 32, 48), [[64, 16]], 0, 0)
+    iota(c("CI", 48, 64), [[16, 16]], 4096, 0)
+    iota(c("IO"), [[1, 16]], 0, 0)
+    vts(c("PI", 1, 2), c("PI", 0, 1), 15, None, O.bitwise_and)
+    K = c("COL", 0, 1)
+    vcopy(K, c("PI", 1, 2))
+    act(c("COL", 1, 2), K, AF.Copy, scale=16.0)
+    act(c("COL", 2, 3), K, AF.Copy, scale=4.0)
+    act(c("COL", 3, 4), K, AF.Copy, scale=-1.0)
+    vts(c("COL", 4, 5), K, 15.0, None, O.is_equal)
+    act(c("COL", 5, 6), c("COL", 4, 5), AF.Identity, bias=1.0, scale=-1.0)
+    act(c("COL", 10, 11), K, AF.Sign)
+    act(c("B32", 0, 16), c("CI", 0, 16), AF.Identity, bias=c("COL", 1, 2))
+    act(c("B32", 16, 48), c("CI", 16, 48), AF.Identity, bias=c("COL", 2, 3))
+    act(c("B32", 48, 64), c("CI", 48, 64), AF.Identity, bias=K)
+    act(c("BW0"), c("B32", 0, BW_), AF.Copy)
+    asel(c("BDa"), c("ON", 0, 128), [[-16, 8], [0, 16]], O.is_ge, 0, 1)
+    asel(c("BD"), c("BDa"), [[16, 8], [0, 16]], O.is_ge, 15, -1)
+    asel(c("ID"), c("ON", 0, 128), [[-1, 128]], O.is_equal, 0, 1)
+    asel(c("TI"), c("BD"), [[1, 128]], O.is_ge, 0, -1)
+    asel(c("TS"), c("BD"), [[1, 128]], O.is_gt, 0, -1)
+    vset(c("AD", 0, 512), 1.0, 0.5)
+    vts(raw(T.TRIM[:, 0, :], "TRIM", 0, 16, True), c("IO"), K, None, O.is_gt)
+    for n in (1, 2, 4, 8):
+        vcopy(raw(T.TRIM[:, n:2 * n, :], "TRIM", 16 * n, 32 * n, True), raw(T.TRIM[:, 0:n, :], "TRIM", 0, 16 * n))
+    for nm, src, v in (("NI", "ID", -1.0), ("I8", "ID", 8192.0), ("N8", "ID", -8192.0), ("HI", "ID", 0.5), ("QI", "ID", -0.25), ("HN", "ID", -0.5),
+                       ("NBD", "BD", -1.0), ("FE", "F", c("COL", 10, 11))):
+        act(c(nm), c(src), AF.Copy, scale=v)
+    vcopy(c("IDh"), c("ID"), k=0.5)
+    vts(c("NIh"), c("ID"), -1.0, None, O.mult, k=0.5)
+    act(c("R15"), c("ON", 0, 128), AF.Copy, scale=c("COL", 4, 5))
+    for k in range(4):
+        vset(c("SM", BL * 4 * k, BL * 4 * k + BL * 4), 1.0, 0.5)
+    vset(c("SM", 15, BL * 16, 16), 0.0)
+    for b in range(NB):
+        vset(c("PM", b * WB + 16, b * WB + 32), 0.0, 0.5)
+    vcopy(c("L"), c("LI"))
+    vcopy(c("E"), c("EI"))
+    vts(c("K2"), c("ON", 0, 128), 2048.0, None, O.mult, k=0.5)
+    vts(c("COL", 6, 7), c("TH", 0, 1), -1.0, -0.5, O.mult, O.add)
+    vtt(c("COL", 7, 8), c("COL", 6, 7), c("COL", 5, 6), O.mult)
+    vtt(c("COL", 8, 9), c("COL", 7, 8), c("COL", 4, 5), O.add)
+    vts(c("COL", 9, 10), c("TH", 1, 2), -1.0, -0.5, O.mult, O.add)
+    KN, T0, T1 = c("COL", 3, 4), c("COL", 8, 9), c("COL", 9, 10)
+
+    def sel(name, m):
+        return c(name, 16 - m, 144 - m)
+
+    def wrap(out, name, v, lo, hi, first=None):
+        lst = list(first or [])
+        for m in range(16):
+            lst.append((out, sel(name, m), c(v, lo + m, hi, 16), not lst, m == 15))
+        mm(lst)
+
+    for t in range(STEPS):
+        f, back, last = (rank + 1 + t % 3) % 4, (rank - 1 - t % 3) % 4, t == STEPS - 1
+        rot = [0]
+        NU, RQ = [c(x, 16 * t, 16 * t + 16) for x in ("NU", "RQ")]
+        RP, BU = [c(x, NC * t, NC * t + NC) for x in ("RP", "BU")]
+        wrap(c("psU", 0, 16), "WF", "Q2", 0, NC)
+        vcopy(c("UI"), c("psU", 0, 16))
+        vts(c("U"), c("UI"), 4095, None, O.bitwise_and)
+        vtt(c("US"), c("U"), c("U"), O.mult)
+        vts(c("SH"), c("US"), 5, None, O.arith_shift_right)
+        if t:
+            vts(c("T37"), c("U"), 37.0, c("AC"), O.mult, O.add)
+        else:
+            vts(c("T37"), c("U"), 37.0, None, O.mult)
+        vtt(c("NN"), c("SH"), c("T37"), O.add)
+        vts(c("N"), c("NN"), 4095, None, O.bitwise_and)
+        vcopy(NU, c("N"))
+        so = send(f, NU, RQ, "rq%d" % t)
+        if t == 0:
+            for k in range(4):
+                asel(c("ETb", 512 * k, 512 * k + 512), c("AD", 0, 512), [[-1, 4], [-16, 8], [0, 16]], O.is_equal, -4 * k, 1, deps=(so,))
+                vcopy(c("ET", 512 * k, 512 * k + 512), c("ETb", 512 * k, 512 * k + 512), k=0.5)
+        vcopy(c("LG"), ind(c("D", 0, 4096), NU))
+        wrap(c("psW", 0, 16), "F0h", "LG", 0, NC)
+        vcopy(c("LU"), c("psW", 0, 16))
+        vcopy(c("PU"), ind(c("L"), c("LU")))
+        for a in range(0, NC, CH):
+            y0 = a // BL * WB + 16 + 16 * (a % BL)
+            act(c("XG", y0, y0 + 16 * CH), ind(c("X"), c("PU", a, a + CH)), AF.Copy)
+        vts(c("PH"), c("PU"), -2048.0, None, O.add, k=0.5)
+        vcopy(c("SG"), ind(c("D", 0, 4096), RQ))
+        wrap(c("psU", 32, 48), "F0h", "SG", 0, NC)
+        vcopy(c("LS"), c("psU", 32, 48))
+        vcopy(RP, ind(c("L"), c("LS")))
+        send(back, RP, BU, "bu%d" % t)
+        vts(c("BH"), BU, -2048.0, None, O.add, k=0.5)
+        vts(c("LO", 0, 16), c("U"), 15, None, O.bitwise_and)
+        vts(c("LO", 16, 32), c("U"), 3, None, O.bitwise_and)
+        vtt(c("CF"), c("LO"), c("B32", 0, 32), O.add)
+        vcopy(c("CU"), c("CF"))
+        act(c("OLD"), ind(c("X"), c("CU", 0, 16)), AF.Copy)
+        if not last:
+            vts(c("NW"), c("N"), -2048.0, None, O.add)
+            vcopy(c("NH", 0, 16), c("NW"))
+            vtt(c("NH", 16, 32), c("LO", 16, 32), c("B32", 32, 48), O.add)
+            mm([(c("psE", m, 512, 16), c("ET", 128 * m, 128 * m + 128), c("NH"), True, True) for m in range(16)])
+            vcopy(c("NR"), c("psE", 0, 256))
+            act(c("CV"), c("psE", 256, 512), AF.Copy)
+            for k in range(16):
+                n = 256 - 16 * k
+                vts(raw(T.EQ[:, k, 0:n], "EQ", 256 * k, 256 * k + n, True), c("NR", 16 * k, 256), c("NW", k, k + 1), None, O.is_equal, k=0.5)
+            dia = raw(T.EQ[:, :, 0:16], "EQ", 0, 4096)
+            add("v", FX + 512 * CY, dia, dia + raw(None, "TRIM", 0, 256), lambda: g.vector.tensor_tensor(
+                out=T.EQ[:, :, 0:16], in0=T.EQ[:, :, 0:16], in1=T.TRIM[:, :, :], op=O.mult))
+            mm([(c("psE", 16 * k, 256), c("BD"), raw(T.EQ[:, k, 0:256 - 16 * k], "EQ", 256 * k, 256 * k + 256 - 16 * k, True), k == 0, k == 15)
+                for k in range(16)])
+            act(c("CB"), c("psE", 0, 256), AF.Copy)
+            wrap(c("psE", 256, 272), "F0", "CB", 0, NC)
+            vts(c("FL"), c("psE", 256, 272), 1.0, None, O.min)
+            vtt(c("DO"), c("FL"), c("B32", 48, 64), O.mult)
+            vtt(c("DO"), c("DO"), c("N"), O.max)
+            vcopy(c("DU"), c("DO"))
+            vcopy(ind(c("D"), c("DU")), c("CV"))
+        for b in range(NB):
+            i0, i1, n0 = b * BL, (b + 1) * BL, 2 * b * BL
+            mm([(c("psW", n0, n0 + BL), c("IDh"), c("BH", i0, i1), True, False), (c("psW", n0, n0 + BL), c("NIh"), c("PH", i0, i1), False, True),
+                (c("psW", n0 + BL, n0 + 2 * BL), c("IDh"), c("PH", i0, i1), True, False),
+                (c("psW", n0 + BL, n0 + 2 * BL), c("IDh"), c("K2"), False, True)])
+        for b in range(NB):
+            i0, i1, w0, w1, x0 = b * BL, (b + 1) * BL, b * BW_, (b + 1) * BW_, b * WB
+            bias[0] = STAG * (NB - 1 - b)
+            B = "psB%d" % (b % 2)
+            XG, DF, PM = [c(x, x0 + 16, x0 + 16 + 16 * BL) for x in ("XG", "DF", "PM")]
+            add("v", FX + BL * 8 * CY, c("PM", x0 + 17, x0 + 16 + BL * 16), c("XG", x0 + 16, x0 + 15 + BL * 16) + c("SM", 0, BL * 16 - 1),
+                lambda x0=x0: g.vector.tensor_tensor_scan(
+                    out=T.PM[:, x0 + 17:x0 + 16 + BL * 16], data0=T.XG[:, x0 + 16:x0 + 15 + BL * 16], data1=T.SM[:, 0:BL * 16 - 1],
+                    initial=0.0, op0=O.max, op1=O.mult))
+            for k in range(BL // CH):
+                a, e, y0, y1 = i0 + k * CH, i0 + k * CH + CH, x0 + 16 + 16 * k * CH, x0 + 16 + 16 * (k + 1) * CH
+                vtt(c("DF", y0, y1), ind(c("X"), c("BU", NC * t + a, NC * t + e)), c("XG", y0, y1), O.subtract)
+                o = c(B, k * CH, k * CH + CH)
+                act(c("AD", 16 * a, 16 * e), c("DF", y0, y1), AF.Abs)
+                mm([(o, sel("F", m), c("AD", 16 * a + m, 16 * e, 16), m == 0, m == 15) for m in range(16)])
+            act(c("S1", i0, i1), c(B, 0, BL), AF.Sign, bias=T0)
+            mm([(c(B, 128, 128 + BL), c("TI"), c("S1", i0, i1), True, True),
+                (c(B, 256, 256 + BL), c("TS"), c("S1", i0, i1), True, False),
+                (c(B, 256, 256 + BL), c("NI"), c("ON", 0, BL), False, True)])
+            act(c("AL", 2 * i0, 2 * i1), c(B, 128, 128 + 2 * BL), AF.Relu, bias=KN, scale=-1.0)
+            LT, LE = c("AL", 2 * i0, 2 * i0 + BL), c("AL", 2 * i0 + BL, 2 * i1)
+            wrap(c(B, 0, BW_), "F", "AL", 2 * i0, 2 * i0 + BL, [(c(B, 0, BW_), c("ID"), c("BW0"), True, False)])
+            OF = c("OF", w0, w1)
+            vcopy(OF, c(B, 0, BW_))
+            d, xs, ds, ml = c("d", i0, i1), c("XS", i0, i1), c("DS", i0, i1), c("ML", i0, i1)
+            vtt(c("MG", i0, i1), ind(PM, OF), c("QB", i0, i1), O.subtract)
+            act(d, c("MG", i0, i1), AF.Abs)
+            act(xs, ind(XG, OF), AF.Copy)
+            act(ds, ind(DF, OF), AF.Copy)
+            px, py, pl = c(B, 128, 128 + BL), c(B, 128 + BL, 128 + 2 * BL), c(B, 384, 384 + BL)
+            mm([(px, c("ID"), xs, True, False), (px, c("NI"), d, False, True),
+                (py, c("ID"), xs, True, False), (py, c("ID"), ds, False, False), (py, c("NI"), d, False, True)])
+            act(c("AB", 2 * i0, 2 * i1), c(B, 128, 128 + 2 * BL), AF.Abs)
+            mm([(pl, c("NBD"), c("AB", 2 * i0, 2 * i0 + BL), True, False), (pl, c("I8"), LT, False, False),
+                (pl, c("BD"), c("AB", 2 * i0 + BL, 2 * i1), False, True)])
+            vts(ml, pl, 0.0, None, O.is_lt)
+            vtt(c("ZD", i0, i1), c("psW", 2 * i0, 2 * i0 + BL), ml, O.mult)
+            vtt(c("ZN", i0, i1), c("psW", 2 * i0 + BL, 2 * i1), c("ZD", i0, i1), O.add)
+            vcopy(c("ZU", i0, i1), c("ZN", i0, i1))
+            vtt(c("EZ", i0, i1), c("ZN", i0, i1), c("E", i0, i1), O.subtract)
+            for k in range(BL // CH):
+                a, e = i0 + k * CH, i0 + k * CH + CH
+                if G3V[b][k]:
+                    vcopy(c("ZG", 16 * a, 16 * e), ind(c("X"), c("ZU", a, e)))
+                else:
+                    act(c("ZG", 16 * a, 16 * e), ind(c("X"), c("ZU", a, e)), AF.Copy)
+            ox, part = c(B, 0, BL), []
+            for h in range(4):
+                Z, a = "psZ%d" % (rot[0] % 3), 16 * i0 + 4 * BL * h
+                rot[0] += 1
+                mm([x for j in range(4) for x in ((c(Z, BL * j, BL * j + BL), c("NI"), d, True, False),
+                                                  (c(Z, BL * j, BL * j + BL), c("ID"), c("ZG", 16 * i0 + 4 * h + j, 16 * i1, 16), False, True))])
+                act(c("AX", a, a + 512), c(Z), AF.Abs)
+                part.append(mm([(ox, sel("F", m), c("AX", 16 * i0 + BL * m, 16 * i0 + BL * m + BL), m == 0, False) for m in range(4 * h, 4 * h + 4)], after=part[:1]))
+            mm([(ox, c("N8"), LE, False, True)], after=part)
+            act(c("S2", i0, i1), ox, AF.Sign, bias=T1)
+            o, oe = c(B, 256, 256 + BL), c(B, 384, 384 + BW_)
+            mm([(o, c("TI"), c("S2", i0, i1), True, True)])
+            act(c("A2", i0, i1), o, AF.Relu, bias=KN, scale=-1.0)
+            wrap(oe, "FE", "A2", i0, i1, [(oe, c("ID"), c("BW0"), True, False)])
+            vcopy(c("OE", w0, w1), oe)
+            act(c("XL", i0, i1), ind(c("ZG", 16 * i0, 16 * i1), c("OE", w0, w1)), AF.Copy)
+            mm([(ox, c("ID"), d, True, False), (ox, c("HN"), c("ON", 0, BL), False, False), (ox, c("ID"), c("XL", i0, i1), False, True)])
+            vts(c("Q2", i0, i1), ox, 16777216.0, 16777216.0, O.add, O.subtract)
+            act(c("QB", i0, i1), c("Q2", i0, i1), AF.Copy, scale=0.5)
+        bias[0] = 0.0
+        if not last:
+            mm([(c("psU", 128, 128 + BL), c("R15"), c("ML", b * BL, b * BL + BL), b == 0, b == NB - 1) for b in range(NB)])
+            act(c("JK", 0, BL), c("psU", 128, 128 + BL), AF.Copy, accum=c("AC"))
+        mm([(c("psE", 0, NC), c("HI"), c("OLD"), True, False), (c("psE", 0, NC), c("HI"), c("d"), False, False),
+            (c("psE", 0, NC), c("QI"), c("ON"), False, True)])
+        vts(c("NX"), c("psE", 0, NC), 8388608.0, 8388608.0, O.add, O.subtract)
+        vcopy(ind(c("X"), c("CU", 0, 16)), c("NX"))
+        if last:
+            dma("y", dram(T.yx[:, :]), c("X"), 4.0)
+        for b in range(NB):
+            i0, i1 = b * BL, (b + 1) * BL
+            vtt(c("EM", i0, i1), c("A2", i0, i1), c("EZ", i0, i1), O.mult)
+            vtt(c("E", i0, i1), c("E", i0, i1), c("EM", i0, i1), O.add)
+            vcopy(ind(c("L", 4 * i0, 4 * i1), c("CU", 16 + i0 // 16, 16 + i1 // 16)), c("E", i0, i1))
+            if last:
+                dma("y", dram(T.yl[:, 4 * i0:4 * i1]), c("L", 4 * i0, 4 * i1), 3.0)
+    dma("s", dram(T.yq[:, :]), c("QB"), 2.0)
+    return ops
+
+
+def sgs(dur, queue, pred, succ, pri):
+    n = len(dur)
+    left, at, fin, qfree, ready, order = [len(p) for p in pred], [0.0] * n, [0.0] * n, {}, {}, []
+    for i in range(n):
+        if not left[i]:
+            ready.setdefault(queue[i], []).append((0.0, i))
+    for _ in range(n):
+        s, q = min((max(qfree.get(q, 0.0), min(lst)[0]), q) for q, lst in ready.items() if lst)
+        _, i, x = max((pri[j], -j, y) for y, j in ready[q] if y <= s + LOOK)
+        i = -i
+        ready[q].remove((x, i))
+        fin[i] = qfree[q] = max(x, qfree.get(q, 0.0)) + dur[i]
+        order.append(i)
+        for k, w in succ[i]:
+            left[k] -= 1
+            at[k] = max(at[k], fin[i] + w)
+            if not left[k]:
+                ready.setdefault(queue[k], []).append((at[k], k))
+    return order, fin
+
+
+def tweak(pri, seed, amp):
+    out = []
+    for i, p in enumerate(pri):
+        h = (i * 2654435761 + seed * 40503 + (i * i + seed) * 97) % 1000003
+        out.append(p + amp * (h / 500001.5 - 1.0) if h % 7 == seed % 7 else p)
+    return out
+
+
+def schedule(ops):
+    n = len(ops)
+    dur, queue = [o["dur"] for o in ops], [o["q"] for o in ops]
+    pred, succ, pri = [[] for _ in ops], [[] for _ in ops], [0.0] * n
+    for i, o in enumerate(ops):
+        for d in o["hard"] + o["soft"]:
+            w = 0.0 if d in o["soft"] else ops[d]["lat"] + (WAKE if ops[d]["q"] != o["q"] else 0.03)
+            pred[i].append((d, w))
+            succ[d].append((i, w))
+    for i in range(n - 1, -1, -1):
+        pri[i] = dur[i] + max([pri[k] + w for k, w in succ[i]] or [0.0])
+    pri = [pri[i] + ops[i]["bias"] + NOISE * ((i * 7919 + SEED * 104729 + (i * SEED * 31) % 1013) % 1009) / 1009 for i in range(n)]
+    best = None
+    for _ in range(ROUNDS):
+        order, fin = sgs(dur, queue, pred, succ, pri)
+        end = max(fin[i] + ops[i]["lat"] for i in range(n))
+        if best is None or end < best[0]:
+            best = (end, order, list(pri))
+        _, pri = sgs(dur, queue, succ, pred, fin)
+    order, pri = best[1], best[2]
+    for seed, amp in TWEAKS:
+        pri = tweak(pri, seed, amp)
+    return sgs(dur, queue, pred, succ, pri)[0], pri
+
+
+def emit(g, T, ops, order):
+    qs = {"v": (g.vector, "cv"), "s": (g.scalar, "cs"), "t": (g.tensor, "ct"), "g": (g, "cg"), "y": (g.sync, None)}
+    cnt, known, snap, mark = {}, {}, {}, {}
+    for i in order:
+        o = ops[i]
+        q, kn = o["q"], known.setdefault(o["q"], {})
+        if o["call"] is not None:
+            need = {}
+            for d in o["hard"]:
+                s, v = mark[d]
+                if kn.get(s, 0) < v and (s not in need or need[s][0] < v):
+                    need[s] = (v, d)
+            for s in list(need):
+                if any(s2 != s and snap[need[s2][1]].get(s, 0) >= need[s][0] for s2 in need):
+                    del need[s]
+            for s, (v, d) in sorted(need.items()):
+                qs[q][0].wait_ge(T.sem[s], v)
+                kn[s] = v
+                for s2, v2 in snap[d].items():
+                    kn[s2] = max(kn.get(s2, 0), v2)
+            r = o["call"]()
+        s = o["sem"]
+        if s is None:
+            s = qs[q][1]
+            r.then_inc(T.sem[s], 1)
+        cnt[s] = cnt.get(s, 0) + o["n"]
+        mark[i] = (s, cnt[s])
+        snap[i] = dict(kn) if o["call"] is not None else {}
+    for s in sorted(cnt):
+        if known.get("g", {}).get(s, 0) < cnt[s]:
+            g.wait_ge(T.sem[s], cnt[s])
+
+
+def rank_program(g, core, T, topo):
+    if T.rank_of(core) is None:
+        return
+    ops = program(g, core, T, topo)
+    emit(g, T, ops, schedule(ops)[0])

@@ -2,38 +2,41 @@ from concourse.mybir import AluOpType as O, ActivationFunctionType as AF
 
 NC, CH, BL, STEPS = 256, 64, 128, 4
 NB, BW_ = NC // BL, BL // 16
+GR = 1 + 2 * BL
 WB = BL * 16 + 32
 f32, bf, i32, u16, f16 = "float32", "bfloat16", "int32", "uint16", "float16"
 SCRATCH = {}
-for _dt, _names in ((bf, "X:4096 XG:%d DF:%d PM:%d AD:4096 AX:4096 ZG:4096 d:256 SM:%d QB:256 Q2:256 W1:1 ON:256 G8:24 F:144 F0:144 FE:144 "
-                     "WF:144 BDa:128 BD:128 NBD:128 ID:128 NI:128 I8:128 N8:128 HI:128 QI:128 HN:128 TI:128 TS:128 R15:128 ETb:2048 BW0:8 OLD:256 NX:256 "
-                     "CB:256 S1:256 AL:512 MG:256 XS:256 DS:256 XL:256 AB:512 ML:256 S2:256 A2:256 JK:128" % (NB * WB, NB * WB, NB * WB, BL * 16)),
-                    (f32, "L:1024 E:256 COL:16 IO:16 CI:64 B32:64 T37:16 CF:32 NW:16 CV:256 FL:16 DO:16 ZD:256 ZN:256 EZ:256 EM:256 AC:1"),
-                    (i32, "D:4352 LI:1024 EI:256 TH:2 PI:2 UI:16 U:16 US:16 SH:16 NN:16 N:16 LO:32"),
-                    (u16, "ZU:256 NU:64 RQ:64 RP:1024 BU:1024 LU:16 LS:16 PU:256 CU:32 DU:16 OF:16 OE:16"),
-                    (f16, "F0h:144 ET:2048 LG:256 SG:256 NH:32 NR:256 PH:256 BH:256 K2:128 IDh:128 NIh:128")):
+for _dt, _names in ((bf, "X:4096 PM:%d AD:4096 AX:4096 AY:4096 d:256 SM:1024 SM2:256 QB:256 W1:1 ON:256 G8:32 G2:8 GN:8 F:144 F0:144 NF:144 F8:144 "
+                     "FY:144 FD:144 WF:144 BDa:128 BD:128 NBD:128 ID:128 NI:128 N8:128 HI:128 QI:128 SH:128 P4:128 N4:128 R15:128 ETb:2048 BW0:16 "
+                     "TT0:128 TT1:256 OLD:256 NX:256 EQ:256 SC1:256 SC2:512 GE:256 MG:256 XS:256 DS:256 XL:512 AB:512 SG1:256 NA:512 INJ:128 JK:128" % (NB * WB)),
+                    (f32, "L:1024 L2:3072 Z2:1536 COL:16 IO:256 CI:64 B32:32 NR:512 CF:32 A1:16 V2:16 ZD:256 ZE:512 EZ:256 AC:1 TF:6"),
+                    (i32, "D:4112 DO:1024 DI:1024 LI:1024 LJ:1024 EI:256 TH:2 TI:4 PI:2 UI:16 U:16 V3:16 NL:48"),
+                    (u16, "NU:16 BU:256 LU:16 LS:16 PU:256 CU:64 C2:48 DU:32 OF:16 OE:32 GL:16"),
+                    (f16, "F0h:144 F1h:144 ET:2048 LG:256 SG:256 NH:32 PH:256 BH:256 K2:128 IDh:128 HIh:128 HNh:128 TR:512")):
     for _x in _names.split():
         SCRATCH[_x.split(":")[0]] = ("sbuf", [128, int(_x.split(":")[1])], _dt)
-SCRATCH["EQ"] = ("sbuf", [128, 16, 256], bf)
-SCRATCH["TRIM"] = ("sbuf", [128, 16, 16], bf)
-for _p in ("psU", "psW", "psE", "psB0", "psB1", "psZ0", "psZ1", "psZ2"):
+SCRATCH["G"] = ("sbuf", [128, NB * GR * 16], bf)
+for _p in ("psU", "psE", "psD", "psB0", "psB1", "psZ0", "psZ1", "psZ2"):
     SCRATCH[_p] = ("psum", [128, 512], f32)
-SEMAPHORES = ["cv", "cs", "ct", "cg", "ls"] + ["dma%d" % k for k in range(16)] + ["%s%d" % (x, k) for x in ("rq", "bu") for k in range(STEPS)]
+SEMAPHORES = ["cv", "cs", "ct", "cg"] + ["dma%d" % k for k in range(24)] + ["%s%d" % (x, k) for x in ("ls", "rs") for k in range(17)]
 
-CY, PEC, GA, SC, FX, WAKE, HOP, RISS = 0.00095, 0.0005, 1.5, 3.5, 0.065, 0.06, 1.6, 0.5
-G3V = ((1, 0), (1, 0))
-TWEAKS = ((44348, 0.7), (22955, 0.7), (83941, 1.5), (59513, 0.7), (97583, 0.3), (82455, 0.3), (77474, 0.3), (72586, 0.3), (51897, 0.3),
-          (99409, 1.5), (6188, 0.7), (51193, 0.3), (58577, 0.7), (57939, 0.3), (27328, 1.5), (8204, 0.3), (37839, 0.3))
-STAG, SEED, NOISE, ROUNDS, LOOK = 0.5, 295390, 2, 12, 0.05
+CY, PEC, GA, SC, FX, WAKE, HOP, RISS = 0.00095, 0.0005, 1.5, 3.5, 0.055, 0.06, 2.0, 0.5
+FORM = ("df", "z")
+PART = ("t", "vp")
+BK1, BK2 = ("psD", "psZ2"), ("psZ0", "psZ1")
+STAG, EARLY, ROUNDS, SEED, ORDER = 0.5, 0.0, 4000, 1, []
 
 
 def program(g, core, T, topo):
     rank, ops, acc = T.rank_of(core), [], {}
-    nsem, bias = [0], [0.0]
+    nsem, bias = [0, 0], [0.0]
 
     def c(name, lo=0, hi=None, st=1):
         hi = SCRATCH[name][1][-1] if hi is None else hi
         return [(T[name][:, lo:hi:st] if st > 1 else T[name][:, lo:hi], name, lo, hi, st == 1, (hi - lo + st - 1) // st)]
+
+    def gv(r0, r1, k=0, st=1):
+        return c("G", 16 * r0 + k, 16 * r1, st)
 
     def raw(ap, name, lo, hi, full=False):
         return [(ap, name, lo, hi, full, hi - lo)]
@@ -78,7 +81,7 @@ def program(g, core, T, topo):
 
     def vtt(out, a, b, op):
         ps = a[0][1][:2] == "ps" or b[0][1][:2] == "ps"
-        return add("v", cost(out, a, 1.0 if ps else 2.0), out, a + b,
+        return add("v", cost(out, a, 1.0 if ps else 2.0), out[:1], a + b + out[1:],
                    lambda: g.vector.tensor_tensor(out=out[0][0], in0=a[0][0], in1=b[0][0], op=op))
 
     def vts(out, a, s1, s2, o0, o1=None, k=1.0):
@@ -91,6 +94,10 @@ def program(g, core, T, topo):
     def vset(out, v, k=1.0):
         return add("v", cost(out, None, k), out, [], lambda: g.vector.memset(out[0][0], v))
 
+    def scan(out, a, mask, k):
+        return add("v", cost(out, None, k), out, a + mask, lambda: g.vector.tensor_tensor_scan(
+            out=out[0][0], data0=a[0][0], data1=mask[0][0], initial=0.0, op0=O.max, op1=O.mult))
+
     def act(out, a, fn, bias=None, scale=None, accum=None):
         kw = {}
         if bias is not None:
@@ -99,7 +106,7 @@ def program(g, core, T, topo):
             kw["scale"] = scale[0][0] if isinstance(scale, list) else scale
         if accum is not None:
             kw["accum_out"] = accum[0][0]
-        return add("s", cost(out, a, 1.0) + 0.02, out + (accum or []), a + [x for s in (bias, scale) if isinstance(s, list) for x in s],
+        return add("s", cost(out, a, 1.0) + 0.015, out + (accum or []), a + [x for s in (bias, scale) if isinstance(s, list) for x in s],
                    lambda: g.scalar.activation(out=out[0][0], in_=a[0][0], func=fn, **kw))
 
     def mm(lst, after=()):
@@ -108,7 +115,13 @@ def program(g, core, T, topo):
             for (o, l, r, s, e) in lst:
                 x = g.tensor.matmul(out=o[0][0], lhsT=l[0][0], rhs=r[0][0], start=s, stop=e)
             return x
-        return add("t", 0.08 + sum(max(64, x[2][0][5]) for x in lst) * PEC, [lst[0][0][0]], [v for x in lst for v in x[1] + x[2]], call, after=after)
+        return add("t", 0.03 + sum(max(64, x[2][0][5]) for x in lst) * PEC, [lst[0][0][0]], [v for x in lst for v in x[1] + x[2]], call, after=after)
+
+    def grp(parts, lst, last=False):
+        parts.append(mm([x + (not parts and n == 0, last and n == len(lst) - 1) for n, x in enumerate(lst)], after=parts if last else parts[:1]))
+
+    def one(lst):
+        grp([], lst, True)
 
     def dma(q, out, a, us, calls=None):
         s = "dma%d" % nsem[0]
@@ -120,19 +133,24 @@ def program(g, core, T, topo):
                 {"y": g.sync, "s": g.scalar}[q].dma_start(o, i).then_inc(T.sem[s], 16)
         return add(q, 0.1 * len(lst), out, a, call, sem=s, n=16 * len(lst), lat=us)
 
-    def send(to, src, dst, sem):
+    def send(to, src, dst, us=0.0):
         to = T.cores[to]
         if not topo.may_write(core, to):
             raise ValueError("this core may not write to core %d" % to)
-        eng = topo.engines(core, to)[::2]
+        eng = topo.engines(core, to)
         mask = sum(1 << e for e in eng)
         rid, pid = topo.addr(to)[:2]
+        ls, rs = "ls%d" % nsem[1], "rs%d" % nsem[1]
+        nsem[1] += 1
 
         def call():
-            g.remote_dma(dst[0][0], src[0][0], T.sem[sem], T.sem["ls"], pid, rid, mask)
-        o = add("g", RISS, [], src, call, sem="ls", n=len(eng))
-        add("r" + sem, 0.0, dst, [], None, sem=sem, n=len(eng), deps=(o,), lat=HOP)
+            g.remote_dma(dst[0][0], src[0][0], T.sem[rs], T.sem[ls], pid, rid, mask)
+        o = add("g", RISS, [], src, call, sem=ls, n=len(eng), lat=HOP + us - RISS)
+        add(rs, 0.0, dst, [], None, sem=rs, n=len(eng), deps=(o,))
         return o
+
+    def reader(t):
+        return (rank - 1 - t % 3) % 4
 
     def dram(ap):
         return [(ap, None, 0, 0, False, 0)]
@@ -156,259 +174,326 @@ def program(g, core, T, topo):
     asel(c("G8", 0, 8), c("ON", 0, 8), [[-16, 8]], O.is_ge, 0, 1)
     asel(c("G8", 8, 16), c("G8", 0, 8), [[16, 8]], O.is_ge, 15, -1)
     asel(c("G8", 16, 24), c("ON", 0, 8), [[-16, 8]], O.is_equal, 0, 1)
+    G1 = c("G8", 8, 16)
     bias[0] = 100.0
     vset(c("D", 0, cut), 0.0)
-    iota(c("D", cut, 4352), [[0, 4352 - cut]], 0, 0)
-    dma("y", raw(T.D[0:128:16, 0:4096], "D", 0, 4096), dram(T.dr[:, :]), 2.5)
-    vcopy(c("F", 16, 144, 16), c("G8", 8, 16))
-    vcopy(c("F0", 16, 144, 16), c("G8", 16, 24))
-    vts(c("WF"), c("F"), c("W1"), 0.5, O.mult, O.mult)
-    vcopy(c("F0h"), c("F0"))
-    act(c("Q2"), c("QB"), AF.Copy, scale=2.0)
-    bias[0] = 0.0
+    iota(c("D", cut, 4112), [[0, 4112 - cut]], 0, 0)
+    DROW = [raw(T.D[j:128:16, 0:4096], "D", 0, 4096) for j in range(2)]
+    dma("y", c("DO", 0, 256), dram(T.dr[:, :]), 2.2)
     dma("s", c("LI"), dram(T.lg[:, :]), 3.0)
+    dma("y", DROW[0], dram(T.dr[:, :]), 2.5)
+    send(reader(0), c("DO", 0, 256), c("DI", 0, 256), 2.0)
+    so = send(reader(0), c("LI"), c("LJ"), 3.0)
+    vcopy(c("F", 16, 144, 16), G1)
+    vcopy(c("F0", 16, 144, 16), c("G8", 16, 24))
+    vts(c("WF"), c("F"), c("W1"), None, O.mult)
+    vcopy(c("F0h"), c("F0"))
+    bias[0] = 0.0
+    asel(c("G8", 24, 32), c("ON", 0, 8), [[-16, 8]], O.is_equal, -1, 1)
+    vset(c("F1h"), 0.0, 0.5)
+    vcopy(c("F1h", 16, 144, 16), c("G8", 24, 32))
     for k in range(2):
         dma("ys"[k], c("X", 2048 * k, 2048 * k + 2048), dram(T.xr[:, 2048 * k:2048 * k + 2048]), 4.0)
     dma("s", c("EI"), dram(T.e0[:, :]), 4.0)
     dma("y", raw(T.TH[:, :], "TH", 0, 2, True), dram(None), 4.0, [(T.TH[j:128:16, :], T.th[:, :]) for j in range(16)])
     iota(c("PI", 0, 1), [[0, 1]], 0, 1)
-    iota(c("CI", 0, 16), [[256, 16]], 0, 0)
-    iota(c("CI", 16, 32), [[0, NB], [64, BW_]], 0, 0)
-    iota(c("CI", 32, 48), [[64, 16]], 0, 0)
-    iota(c("CI", 48, 64), [[16, 16]], 4096, 0)
-    iota(c("IO"), [[1, 16]], 0, 0)
+    iota(c("CI", 0, 16), [[0, NB], [64, BW_]], 0, 0)
+    iota(c("CI", 16, 32), [[0, NB], [256, BW_]], 0, 0)
+    iota(c("CI", 32, 48), [[-2048, 2], [256, BW_]], 0, 0)
+    iota(c("IO"), [[0, 16], [1, 16]], 0, 0)
+    iota(c("NR", 256, 512), [[4, 256]], 2048, 0)
     vts(c("PI", 1, 2), c("PI", 0, 1), 15, None, O.bitwise_and)
     K = c("COL", 0, 1)
     vcopy(K, c("PI", 1, 2))
     act(c("COL", 1, 2), K, AF.Copy, scale=16.0)
     act(c("COL", 2, 3), K, AF.Copy, scale=4.0)
-    act(c("COL", 3, 4), K, AF.Copy, scale=-1.0)
+    act(c("COL", 3, 4), K, AF.Identity, bias=2048.0)
     vts(c("COL", 4, 5), K, 15.0, None, O.is_equal)
-    act(c("COL", 5, 6), c("COL", 4, 5), AF.Identity, bias=1.0, scale=-1.0)
-    act(c("COL", 10, 11), K, AF.Sign)
-    act(c("B32", 0, 16), c("CI", 0, 16), AF.Identity, bias=c("COL", 1, 2))
-    act(c("B32", 16, 48), c("CI", 16, 48), AF.Identity, bias=c("COL", 2, 3))
-    act(c("B32", 48, 64), c("CI", 48, 64), AF.Identity, bias=K)
-    act(c("BW0"), c("B32", 0, BW_), AF.Copy)
+    for j, v in enumerate((-16.0, -1.0, -12288.0)):
+        vts(c("COL", 5 + j, 6 + j), K, float(j), v, O.is_equal, O.mult)
+    K15 = c("COL", 4, 5)
+    act(c("B32", 0, 16), c("CI", 0, 16), AF.Identity, bias=c("COL", 2, 3))
+    act(c("B32", 16, 32), c("CI", 16, 32), AF.Identity, bias=c("COL", 1, 2))
+    act(c("BW0"), c("CI", 32, 48), AF.Identity, bias=c("COL", 1, 2))
+    vcopy(c("GL"), c("IO", 0, 16))
+    vts(c("NR", 0, 256), c("IO"), K, 8192.0, O.is_le, O.mult)
+    vts(c("TR", 0, 256), c("NR", 0, 256), 2048.0, None, O.add)
+    vcopy(c("TR", 256, 512), c("NR", 256, 512))
     asel(c("BDa"), c("ON", 0, 128), [[-16, 8], [0, 16]], O.is_ge, 0, 1)
     asel(c("BD"), c("BDa"), [[16, 8], [0, 16]], O.is_ge, 15, -1)
     asel(c("ID"), c("ON", 0, 128), [[-1, 128]], O.is_equal, 0, 1)
-    asel(c("TI"), c("BD"), [[1, 128]], O.is_ge, 0, -1)
-    asel(c("TS"), c("BD"), [[1, 128]], O.is_gt, 0, -1)
-    vset(c("AD", 0, 512), 1.0, 0.5)
-    vts(raw(T.TRIM[:, 0, :], "TRIM", 0, 16, True), c("IO"), K, None, O.is_gt)
-    for n in (1, 2, 4, 8):
-        vcopy(raw(T.TRIM[:, n:2 * n, :], "TRIM", 16 * n, 32 * n, True), raw(T.TRIM[:, 0:n, :], "TRIM", 0, 16 * n))
-    for nm, src, v in (("NI", "ID", -1.0), ("I8", "ID", 8192.0), ("N8", "ID", -8192.0), ("HI", "ID", 0.5), ("QI", "ID", -0.25), ("HN", "ID", -0.5),
-                       ("NBD", "BD", -1.0), ("FE", "F", c("COL", 10, 11))):
-        act(c(nm), c(src), AF.Copy, scale=v)
-    vcopy(c("IDh"), c("ID"), k=0.5)
-    vts(c("NIh"), c("ID"), -1.0, None, O.mult, k=0.5)
-    act(c("R15"), c("ON", 0, 128), AF.Copy, scale=c("COL", 4, 5))
+    asel(c("BDa"), c("BD"), [[1, 128]], O.is_equal, -1, -1)
+    vset(c("AX", 0, 512), 1.0, 0.5)
     for k in range(4):
-        vset(c("SM", BL * 4 * k, BL * 4 * k + BL * 4), 1.0, 0.5)
-    vset(c("SM", 15, BL * 16, 16), 0.0)
+        asel(c("ETb", 512 * k, 512 * k + 512), c("AX", 0, 512), [[-1, 4], [-16, 8], [0, 16]], O.is_equal, -4 * k, 1, deps=(so,))
+        vcopy(c("ET", 512 * k, 512 * k + 512), c("ETb", 512 * k, 512 * k + 512), k=0.5)
+    act(c("COL", 8, 9), K15, AF.Copy, scale=16.0)
+    act(c("COL", 9, 10), c("COL", 5, 6), AF.Identity, scale=-1025.0 / 16, bias=-1.0)
+    act(c("COL", 10, 11), c("COL", 5, 6), AF.Identity, scale=-4097.0 / 16, bias=-1.0)
+    asel(c("INJ"), c("BD"), [[1, 128]], O.is_equal, 15, -1)
+    for nm, src, v in (("NI", "ID", -1.0), ("N8", "ID", -8192.0), ("HI", "ID", 0.5), ("QI", "ID", -0.25), ("P4", "ID", 4096.0), ("N4", "ID", -4096.0),
+                       ("NBD", "BD", -1.0), ("SH", "BDa", 8192.0), ("NF", "F", -1.0), ("F8", "F", 8192.0),
+                       ("FY", "F", c("COL", 9, 10)), ("FD", "F", c("COL", 10, 11))):
+        act(c(nm), c(src), AF.Copy, scale=v)
+    act(c("G2"), G1, AF.Copy, scale=2.0)
+    act(c("GN"), G1, AF.Copy, scale=-1.0)
+    act(c("R15"), c("ON", 0, 128), AF.Copy, scale=c("COL", 8, 9))
+    vcopy(c("IDh"), c("ID"), k=0.5)
+    vts(c("HIh"), c("ID"), 0.5, None, O.mult, k=0.5)
+    vts(c("HNh"), c("ID"), -0.5, None, O.mult, k=0.5)
+    vts(c("K2"), c("ON", 0, 128), 2048.0, None, O.mult, k=0.5)
+    vset(c("SM"), 1.0, 0.5)
+    vset(c("SM", 15, 1024, 16), 0.0)
+    vset(c("SM2"), 1.0, 0.5)
+    vset(c("SM2", 1, 256, 32), 0.0)
     for b in range(NB):
         vset(c("PM", b * WB + 16, b * WB + 32), 0.0, 0.5)
+        vset(gv(b * GR, b * GR + 1), 0.0, 0.5)
     vcopy(c("L"), c("LI"))
-    vcopy(c("E"), c("EI"))
-    vts(c("K2"), c("ON", 0, 128), 2048.0, None, O.mult, k=0.5)
-    vts(c("COL", 6, 7), c("TH", 0, 1), -1.0, -0.5, O.mult, O.add)
-    vtt(c("COL", 7, 8), c("COL", 6, 7), c("COL", 5, 6), O.mult)
-    vtt(c("COL", 8, 9), c("COL", 7, 8), c("COL", 4, 5), O.add)
-    vts(c("COL", 9, 10), c("TH", 1, 2), -1.0, -0.5, O.mult, O.add)
-    KN, T0, T1 = c("COL", 3, 4), c("COL", 8, 9), c("COL", 9, 10)
+    vts(c("TI", 0, 2), c("TH"), 4, None, O.arith_shift_right)
+    vts(c("TI", 2, 4), c("TH"), 15, None, O.bitwise_and)
+    vts(c("TF", 0, 2), c("TI", 0, 2), c("COL", 5, 6), None, O.mult)
+    vts(c("TF", 2, 4), c("TI", 2, 4), 0.5, c("COL", 6, 7), O.add, O.mult)
+    vtt(c("TF", 4, 6), c("TF", 0, 2), c("TF", 2, 4), O.add)
+    vtt(c("TF", 0, 1), c("TF", 5, 6), c("COL", 7, 8), O.add)
+    act(c("TT0"), c("BD"), AF.Copy, scale=c("TF", 4, 5))
+    for j in range(2):
+        act(c("TT1", j, 256, 2), c("BD"), AF.Copy, scale=c("TF", 0, 1))
+    ONE = c("ON", 0, 128)
 
     def sel(name, m):
         return c(name, 16 - m, 144 - m)
 
-    def wrap(out, name, v, lo, hi, first=None):
-        lst = list(first or [])
-        for m in range(16):
-            lst.append((out, sel(name, m), c(v, lo + m, hi, 16), not lst, m == 15))
-        mm(lst)
+    def wrap(out, name, v, lo, hi):
+        return [(out, sel(name, m), c(v, lo + m, hi, 16)) for m in range(16)]
+
+    rot = [0]
+
+    def bank(names=("psZ0", "psZ1", "psZ2")):
+        rot[0] += 1
+        return names[rot[0] % len(names)]
 
     for t in range(STEPS):
-        f, back, last = (rank + 1 + t % 3) % 4, (rank - 1 - t % 3) % 4, t == STEPS - 1
-        rot = [0]
-        NU, RQ = [c(x, 16 * t, 16 * t + 16) for x in ("NU", "RQ")]
-        RP, BU = [c(x, NC * t, NC * t + NC) for x in ("RP", "BU")]
-        wrap(c("psU", 0, 16), "WF", "Q2", 0, NC)
+        to, last = reader(t + 1), t == STEPS - 1
+        NU = c("NU")
+        cu, cv = 32 * (t % 2), 32 * ((t + 1) % 2)
+        LT, L2 = (c("L"), c("L2", 1024 * (t - 1), 1024 * t)) if t else (c("LI"), c("LJ"))
+        if not last:
+            send(to, c("L"), c("L2", 1024 * t, 1024 * t + 1024), 3.0)
+        one(wrap(c("psU", 0, 16), "WF", "QB", 0, NC))
         vcopy(c("UI"), c("psU", 0, 16))
         vts(c("U"), c("UI"), 4095, None, O.bitwise_and)
-        vtt(c("US"), c("U"), c("U"), O.mult)
-        vts(c("SH"), c("US"), 5, None, O.arith_shift_right)
+        vts(c("A1"), c("U"), 592.0, None, O.add)
+        vtt(c("V2"), c("A1"), c("A1"), O.mult)
         if t:
-            vts(c("T37"), c("U"), 37.0, c("AC"), O.mult, O.add)
+            vts(c("V3"), c("V2"), c("AC"), 75520.0, O.add, O.add)
         else:
-            vts(c("T37"), c("U"), 37.0, None, O.mult)
-        vtt(c("NN"), c("SH"), c("T37"), O.add)
-        vts(c("N"), c("NN"), 4095, None, O.bitwise_and)
-        vcopy(NU, c("N"))
-        so = send(f, NU, RQ, "rq%d" % t)
-        if t == 0:
-            for k in range(4):
-                asel(c("ETb", 512 * k, 512 * k + 512), c("AD", 0, 512), [[-1, 4], [-16, 8], [0, 16]], O.is_equal, -4 * k, 1, deps=(so,))
-                vcopy(c("ET", 512 * k, 512 * k + 512), c("ETb", 512 * k, 512 * k + 512), k=0.5)
+            vts(c("V3"), c("V2"), 42752.0, None, O.add)
+        N = c("NL", 0, 16)
+        vts(N, c("V3"), 5, 4095, O.arith_shift_right, O.bitwise_and)
+        vcopy(NU, N)
         vcopy(c("LG"), ind(c("D", 0, 4096), NU))
-        wrap(c("psW", 0, 16), "F0h", "LG", 0, NC)
-        vcopy(c("LU"), c("psW", 0, 16))
-        vcopy(c("PU"), ind(c("L"), c("LU")))
+        one(wrap(c("psU", 32, 48), "F0h", "LG", 0, NC))
+        vcopy(c("LU"), c("psU", 32, 48))
+        vcopy(c("PU"), ind(LT, c("LU")))
+        if t == 0:
+            dma("y", DROW[1], c("DI", 0, 256), 2.5)
+            vcopy(c("SG"), ind(c("D", 0, 4096), NU))
+        one(wrap(c("psE", 0, 16), "F1h", "LG" if t else "SG", 0, NC))
+        vcopy(c("LS"), c("psE", 0, 16))
+        vcopy(c("BU"), ind(L2, c("LS")))
         for a in range(0, NC, CH):
-            y0 = a // BL * WB + 16 + 16 * (a % BL)
-            act(c("XG", y0, y0 + 16 * CH), ind(c("X"), c("PU", a, a + CH)), AF.Copy)
+            r0 = a // BL * GR + 1 + a % BL
+            act(gv(r0, r0 + CH), ind(c("X"), c("PU", a, a + CH)), AF.Copy)
+            y0 = a // BL * WB + 17 + 16 * (a % BL)
+            scan(c("PM", y0, y0 + 16 * CH), gv(r0, r0 + CH), c("SM", 0, 16 * CH), 0.5)
         vts(c("PH"), c("PU"), -2048.0, None, O.add, k=0.5)
-        vcopy(c("SG"), ind(c("D", 0, 4096), RQ))
-        wrap(c("psU", 32, 48), "F0h", "SG", 0, NC)
-        vcopy(c("LS"), c("psU", 32, 48))
-        vcopy(RP, ind(c("L"), c("LS")))
-        send(back, RP, BU, "bu%d" % t)
-        vts(c("BH"), BU, -2048.0, None, O.add, k=0.5)
-        vts(c("LO", 0, 16), c("U"), 15, None, O.bitwise_and)
-        vts(c("LO", 16, 32), c("U"), 3, None, O.bitwise_and)
-        vtt(c("CF"), c("LO"), c("B32", 0, 32), O.add)
-        vcopy(c("CU"), c("CF"))
-        act(c("OLD"), ind(c("X"), c("CU", 0, 16)), AF.Copy)
+        vts(c("BH"), c("BU"), -2048.0, None, O.add, k=0.5)
+        vts(c("NL", 16, 32), c("UI"), 3, None, O.bitwise_and)
+        vts(c("NL", 32, 48), c("UI"), 15, None, O.bitwise_and)
+        vtt(c("CF"), c("NL", 16, 48), c("B32"), O.add)
+        vcopy(c("CU", cu, cu + 32), c("CF"))
+        for a in range(0, NC, BL):
+            act(c("OLD", a, a + BL), ind(c("X", 16 * a, 16 * a + 16 * BL), c("CU", cu + 16 + a // 16, cu + 16 + a // 16 + BW_)), AF.Copy)
         if not last:
-            vts(c("NW"), c("N"), -2048.0, None, O.add)
-            vcopy(c("NH", 0, 16), c("NW"))
-            vtt(c("NH", 16, 32), c("LO", 16, 32), c("B32", 32, 48), O.add)
-            mm([(c("psE", m, 512, 16), c("ET", 128 * m, 128 * m + 128), c("NH"), True, True) for m in range(16)])
-            vcopy(c("NR"), c("psE", 0, 256))
-            act(c("CV"), c("psE", 256, 512), AF.Copy)
-            for k in range(16):
-                n = 256 - 16 * k
-                vts(raw(T.EQ[:, k, 0:n], "EQ", 256 * k, 256 * k + n, True), c("NR", 16 * k, 256), c("NW", k, k + 1), None, O.is_equal, k=0.5)
-            dia = raw(T.EQ[:, :, 0:16], "EQ", 0, 4096)
-            add("v", FX + 512 * CY, dia, dia + raw(None, "TRIM", 0, 256), lambda: g.vector.tensor_tensor(
-                out=T.EQ[:, :, 0:16], in0=T.EQ[:, :, 0:16], in1=T.TRIM[:, :, :], op=O.mult))
-            mm([(c("psE", 16 * k, 256), c("BD"), raw(T.EQ[:, k, 0:256 - 16 * k], "EQ", 256 * k, 256 * k + 256 - 16 * k, True), k == 0, k == 15)
-                for k in range(16)])
-            act(c("CB"), c("psE", 0, 256), AF.Copy)
-            wrap(c("psE", 256, 272), "F0", "CB", 0, NC)
-            vts(c("FL"), c("psE", 256, 272), 1.0, None, O.min)
-            vtt(c("DO"), c("FL"), c("B32", 48, 64), O.mult)
-            vtt(c("DO"), c("DO"), c("N"), O.max)
-            vcopy(c("DU"), c("DO"))
-            vcopy(ind(c("D"), c("DU")), c("CV"))
+            bias[0] = EARLY
+            send(to, c("CU", cu, cu + 16), c("C2", 16 * t, 16 * t + 16))
+            vts(c("NH"), c("NL", 0, 32), -2048.0, None, O.add)
+            one([(c("psE"), c("IDh"), c("TR"))] + [(c("psE", m, 512, 16), c("ET", 128 * m, 128 * m + 128), c("NH")) for m in range(16)])
+            act(c("NR"), c("psE"), AF.Copy)
+            vtt(c("EQ"), ind(N, c("GL")), c("NR", 0, 256), O.is_equal)
+            one([(c("psE", 0, 16), c("IDh"), c("NH", 0, 16))] + wrap(c("psE", 0, 16), "F8", "EQ", 0, NC))
+            vts(c("DU", 0, 32, 2), c("psE", 0, 16), c("COL", 3, 4), 2048.0, O.min, O.add)
+            for n in range(15, -1, -1):
+                vcopy(ind(c("D"), c("DU", 2 * n, 2 * n + 1)), c("NR", 256 + 16 * n, 272 + 16 * n))
+            DO, DI = [c(x, 256 * t + 256, 256 * t + 512) for x in ("DO", "DI")]
+            dma("y", DO, DROW[0], 2.5)
+            send(to, DO, DI, 0.8)
+            dma("y", DROW[1], DI, 2.5)
         for b in range(NB):
-            i0, i1, n0 = b * BL, (b + 1) * BL, 2 * b * BL
-            mm([(c("psW", n0, n0 + BL), c("IDh"), c("BH", i0, i1), True, False), (c("psW", n0, n0 + BL), c("NIh"), c("PH", i0, i1), False, True),
-                (c("psW", n0 + BL, n0 + 2 * BL), c("IDh"), c("PH", i0, i1), True, False),
-                (c("psW", n0 + BL, n0 + 2 * BL), c("IDh"), c("K2"), False, True)])
-        for b in range(NB):
-            i0, i1, w0, w1, x0 = b * BL, (b + 1) * BL, b * BW_, (b + 1) * BW_, b * WB
+            i0, i1, w0, w1, x0 = b * BL, (b + 1) * BL, b * BW_, (b + 1) * BW_, b * GR + 1
+            y0, df, B = x0 + BL, FORM[b] == "df", ("psU", "psE")[b]
             bias[0] = STAG * (NB - 1 - b)
-            B = "psB%d" % (b % 2)
-            XG, DF, PM = [c(x, x0 + 16, x0 + 16 + 16 * BL) for x in ("XG", "DF", "PM")]
-            add("v", FX + BL * 8 * CY, c("PM", x0 + 17, x0 + 16 + BL * 16), c("XG", x0 + 16, x0 + 15 + BL * 16) + c("SM", 0, BL * 16 - 1),
-                lambda x0=x0: g.vector.tensor_tensor_scan(
-                    out=T.PM[:, x0 + 17:x0 + 16 + BL * 16], data0=T.XG[:, x0 + 16:x0 + 15 + BL * 16], data1=T.SM[:, 0:BL * 16 - 1],
-                    initial=0.0, op0=O.max, op1=O.mult))
-            for k in range(BL // CH):
-                a, e, y0, y1 = i0 + k * CH, i0 + k * CH + CH, x0 + 16 + 16 * k * CH, x0 + 16 + 16 * (k + 1) * CH
-                vtt(c("DF", y0, y1), ind(c("X"), c("BU", NC * t + a, NC * t + e)), c("XG", y0, y1), O.subtract)
-                o = c(B, k * CH, k * CH + CH)
-                act(c("AD", 16 * a, 16 * e), c("DF", y0, y1), AF.Abs)
-                mm([(o, sel("F", m), c("AD", 16 * a + m, 16 * e, 16), m == 0, m == 15) for m in range(16)])
-            act(c("S1", i0, i1), c(B, 0, BL), AF.Sign, bias=T0)
-            mm([(c(B, 128, 128 + BL), c("TI"), c("S1", i0, i1), True, True),
-                (c(B, 256, 256 + BL), c("TS"), c("S1", i0, i1), True, False),
-                (c(B, 256, 256 + BL), c("NI"), c("ON", 0, BL), False, True)])
-            act(c("AL", 2 * i0, 2 * i1), c(B, 128, 128 + 2 * BL), AF.Relu, bias=KN, scale=-1.0)
-            LT, LE = c("AL", 2 * i0, 2 * i0 + BL), c("AL", 2 * i0 + BL, 2 * i1)
-            wrap(c(B, 0, BW_), "F", "AL", 2 * i0, 2 * i0 + BL, [(c(B, 0, BW_), c("ID"), c("BW0"), True, False)])
-            OF = c("OF", w0, w1)
-            vcopy(OF, c(B, 0, BW_))
-            d, xs, ds, ml = c("d", i0, i1), c("XS", i0, i1), c("DS", i0, i1), c("ML", i0, i1)
-            vtt(c("MG", i0, i1), ind(PM, OF), c("QB", i0, i1), O.subtract)
-            act(d, c("MG", i0, i1), AF.Abs)
-            act(xs, ind(XG, OF), AF.Copy)
-            act(ds, ind(DF, OF), AF.Copy)
-            px, py, pl = c(B, 128, 128 + BL), c(B, 128 + BL, 128 + 2 * BL), c(B, 384, 384 + BL)
-            mm([(px, c("ID"), xs, True, False), (px, c("NI"), d, False, True),
-                (py, c("ID"), xs, True, False), (py, c("ID"), ds, False, False), (py, c("NI"), d, False, True)])
-            act(c("AB", 2 * i0, 2 * i1), c(B, 128, 128 + 2 * BL), AF.Abs)
-            mm([(pl, c("NBD"), c("AB", 2 * i0, 2 * i0 + BL), True, False), (pl, c("I8"), LT, False, False),
-                (pl, c("BD"), c("AB", 2 * i0 + BL, 2 * i1), False, True)])
-            vts(ml, pl, 0.0, None, O.is_lt)
-            vtt(c("ZD", i0, i1), c("psW", 2 * i0, 2 * i0 + BL), ml, O.mult)
-            vtt(c("ZN", i0, i1), c("psW", 2 * i0 + BL, 2 * i1), c("ZD", i0, i1), O.add)
-            vcopy(c("ZU", i0, i1), c("ZN", i0, i1))
-            vtt(c("EZ", i0, i1), c("ZN", i0, i1), c("E", i0, i1), O.subtract)
-            for k in range(BL // CH):
-                a, e = i0 + k * CH, i0 + k * CH + CH
-                if G3V[b][k]:
-                    vcopy(c("ZG", 16 * a, 16 * e), ind(c("X"), c("ZU", a, e)))
+            part = []
+            grp(part, [(c(B, 0, 128), ONE, c("TT0"))])
+            for a in range(0, BL, CH):
+                names = ind(c("X"), c("BU", i0 + a, i0 + a + CH))
+                if df:
+                    vtt(gv(y0 + a, y0 + a + CH), names, gv(x0 + a, x0 + a + CH), O.subtract)
+                    vts(c("AD", 16 * (i0 + a), 16 * (i0 + a + CH)), gv(y0 + a, y0 + a + CH), 0.0, None, O.max, k=0.5)
                 else:
-                    act(c("ZG", 16 * a, 16 * e), ind(c("X"), c("ZU", a, e)), AF.Copy)
-            ox, part = c(B, 0, BL), []
-            for h in range(4):
-                Z, a = "psZ%d" % (rot[0] % 3), 16 * i0 + 4 * BL * h
-                rot[0] += 1
-                mm([x for j in range(4) for x in ((c(Z, BL * j, BL * j + BL), c("NI"), d, True, False),
-                                                  (c(Z, BL * j, BL * j + BL), c("ID"), c("ZG", 16 * i0 + 4 * h + j, 16 * i1, 16), False, True))])
-                act(c("AX", a, a + 512), c(Z), AF.Abs)
-                part.append(mm([(ox, sel("F", m), c("AX", 16 * i0 + BL * m, 16 * i0 + BL * m + BL), m == 0, False) for m in range(4 * h, 4 * h + 4)], after=part[:1]))
-            mm([(ox, c("N8"), LE, False, True)], after=part)
-            act(c("S2", i0, i1), ox, AF.Sign, bias=T1)
-            o, oe = c(B, 256, 256 + BL), c(B, 384, 384 + BW_)
-            mm([(o, c("TI"), c("S2", i0, i1), True, True)])
-            act(c("A2", i0, i1), o, AF.Relu, bias=KN, scale=-1.0)
-            wrap(oe, "FE", "A2", i0, i1, [(oe, c("ID"), c("BW0"), True, False)])
-            vcopy(c("OE", w0, w1), oe)
-            act(c("XL", i0, i1), ind(c("ZG", 16 * i0, 16 * i1), c("OE", w0, w1)), AF.Copy)
-            mm([(ox, c("ID"), d, True, False), (ox, c("HN"), c("ON", 0, BL), False, False), (ox, c("ID"), c("XL", i0, i1), False, True)])
-            vts(c("Q2", i0, i1), ox, 16777216.0, 16777216.0, O.add, O.subtract)
-            act(c("QB", i0, i1), c("Q2", i0, i1), AF.Copy, scale=0.5)
+                    act(gv(y0 + a, y0 + a + CH), names, AF.Copy)
+                    for h in range(a, a + CH, 32):
+                        Z, dif = c(bank(BK1)), []
+                        if FORM[b] == "z":
+                            one([(Z, c("ID"), gv(x0 + h, x0 + h + 32))])
+                            vtt(c("AD", 16 * (i0 + h), 16 * (i0 + h + 32)), gv(y0 + h, y0 + h + 32), Z, O.max)
+                            continue
+                        grp(dif, [(Z, c("NI"), gv(x0 + h, x0 + h + 32))])
+                        grp(dif, [(Z, c("ID"), gv(y0 + h, y0 + h + 32))], True)
+                        act(c("AD", 16 * (i0 + h), 16 * (i0 + h + 32)), Z, AF.Abs)
+            for r0 in {"df": (y0,), "y": (), "z": (x0, y0)}[FORM[b]]:
+                grp(part, [(c(B, k, 128, 16), gv(r0, r0 + BL, k, 16), c("GN")) for k in range(15)])
+            grp(part, [(c(B, k, 128, 16), c("AD", 16 * i0 + k, 16 * i1, 16), G1 if FORM[b] == "y" else c("G2")) for k in range(15)], True)
+            GE = c("GE", i0, i1)
+            scan(c("SC1", i0, i1), c(B, 0, 128), c("SM", 0, 128), 1.0)
+            one([(c(B, 128, 256), c("SC1", i0, i1), c("ID"))])
+            act(GE, c(B, 128, 256), AF.Sign, bias=K15)
+            one([(c(B, 0, BW_), c("ID"), c("BW0", 0, BW_))] + wrap(c(B, 0, BW_), "NF", "GE", i0, i1))
+            OF = c("OF", w0, w1)
+            vts(OF, c(B, 0, BW_), 16.0, None, O.add)
+            vtt(c("MG", i0, i1), ind(c("PM", b * WB + 16, b * WB + 16 + 16 * BL), OF), c("QB", i0, i1), O.subtract)
+            act(c("d", i0, i1), c("MG", i0, i1), AF.Abs)
+        for b in range(NB):
+            i0, i1, w0, w1, x0 = b * BL, (b + 1) * BL, b * BW_, (b + 1) * BW_, b * GR + 1
+            y0, df, B, W = x0 + BL, FORM[b] == "df", "psB%d" % b, ("psU", "psE")[b]
+            bias[0] = STAG * (NB - 1 - b)
+            d, xs, ds, sg, GE, OF, NA = [c(x, i0, i1) for x in ("d", "XS", "DS", "SG1", "GE")] + [c("OF", w0, w1), c("NA", 2 * i0, 2 * i0 + BL)]
+            act(xs, ind(gv(x0, x0 + BL), OF), AF.Copy)
+            act(ds, ind(gv(y0, y0 + BL), OF), AF.Copy)
+            px, py, pl = c(W, 0, BL), c(W, BL, 2 * BL), c(W, 2 * BL, 3 * BL)
+            one([(px, c("ID"), xs), (px, c("NI"), d)])
+            one([(py, c("ID"), ds), (py, c("NI"), d)] + ([(py, c("ID"), xs)] if df else []))
+            nx = c(W, 3 * BL, 4 * BL)
+            one([(nx, c("HI"), c("OLD", i0, i1)), (nx, c("HI"), d), (nx, c("QI"), ONE)])
+            act(c("AB", 2 * i0, 2 * i1), c(W, 0, 2 * BL), AF.Abs)
+            one([(pl, c("NBD"), c("AB", 2 * i0, 2 * i0 + BL)), (pl, c("N8"), GE), (pl, c("BD"), c("AB", 2 * i0 + BL, 2 * i1))])
+            one([(px, c("HIh"), c("BH", i0, i1)), (px, c("HNh"), c("PH", i0, i1))])
+            one([(py, c("HIh"), c("BH", i0, i1)), (py, c("HIh"), c("PH", i0, i1)), (py, c("IDh"), c("K2"))])
+            act(sg, pl, AF.Sign, bias=-8192.5, scale=-1.0)
+            ZN, EM = c("ZE", 2 * i0, 2 * i0 + BL), c("ZE", 2 * i0 + BL, 2 * i1)
+            vtt(c("ZD", i0, i1), px, sg, O.mult)
+            vtt(ZN, py, c("ZD", i0, i1), O.add)
+            vts(c("NX", i0, i1), nx, 8388608.0, 8388608.0, O.add, O.subtract)
+            vcopy(ind(c("X", 16 * i0, 16 * i1), c("CU", cu + 16 + w0, cu + 16 + w1)), c("NX", i0, i1))
+            LB = c("L", 4 * i0, 4 * i1)
+            old = ind(LB, c("CU", cv + w0, cv + w1)) if t else c("EI", i0, i1)
+            vtt(c("EZ", i0, i1), old, ZN, O.subtract)
+            part, ox, oy = [], c(B, 256, 512, 2), c(B, 257, 512, 2)
+            grp(part, [(c(B, 256, 512), ONE, c("TT1"))])
+            grp(part, [(ox, GE, c("SH")), (oy, GE, c("SH"))])
+            if "v" in PART[b]:
+                mm([(c("psD", j, 512, 4), c("ID"), d, True, True) for j in range(4)])
+            if PART[b] in "tu":
+                for o in (256, 257) if PART[b] == "u" else (257,):
+                    grp(part, [(c(B, o + 2 * k, 512, 32), gv(x0, x0 + BL, k, 16), G1) for k in range(1, 16)])
+                    grp(part, [(c(B, o, 512, 2), d, c("NBD"))])
+                grp(part, [(c(B, 257 + 2 * k, 512, 32), gv(y0, y0 + BL, k, 16), c("GN")) for k in range(1, 16)])
+                for k0 in range(4):
+                    Z, a, dif = bank(BK2), 16 * i0 + 4 * BL * k0, []
+                    grp(dif, [(c(Z), c("NI"), gv(x0, x0 + BL, k0, 4))])
+                    grp(dif, [(c(Z, j, 512, 4), c("ID"), d) for j in range(4)], True)
+                    if PART[b] == "u":
+                        vts(c("AX", a, a + 4 * BL), c(Z), 0.0, None, O.max)
+                    else:
+                        act(c("AX", a, a + 4 * BL), c(Z), AF.Abs)
+                    vtt(c("AY", a, a + 4 * BL), gv(y0, y0 + BL, k0, 4), c(Z), O.max)
+                    for j, (A, S) in enumerate((("AX", G1 if PART[b] == "t" else c("G2")), ("AY", c("G2")))):
+                        grp(part, [(c(B, 256 + 2 * (k0 + 4 * h) + j, 512, 32), c(A, a + h, a + 4 * BL, 4), S) for h in range(4) if k0 + h])
+            for j, (r0, A) in enumerate(((x0, "AX"), (y0, "AY")) if PART[b] not in "tu" else ()):
+                if PART[b][j] == "p":
+                    for k0 in range(4):
+                        Z, a, dif = bank(), 16 * i0 + 4 * BL * k0, []
+                        grp(dif, [(c(Z), c("ID"), gv(r, r + BL, k0, 4)) for r in ((x0, y0) if df and j else (r0,))])
+                        grp(dif, [(c(Z, h, 512, 4), c("NI"), d) for h in range(4)], True)
+                        act(c(A, a, a + 4 * BL), c(Z), AF.Abs)
+                        grp(part, [(c(B, 256 + 2 * (k0 + 4 * h) + j, 512, 32), c(A, a + h, a + 4 * BL, 4), G1) for h in range(4) if k0 + h])
+                elif PART[b][j] == "v":
+                    grp(part, [(c(B, 256 + 2 * k + j, 512, 32), gv(r0, r0 + BL, k, 16), c("GN")) for k in range(1, 16)])
+                    grp(part, [(c(B, 256 + j, 512, 2), d, c("NBD"))])
+                    for k0 in range(4):
+                        a = 16 * i0 + 4 * BL * k0
+                        vtt(c(A, a, a + 4 * BL), gv(r0, r0 + BL, k0, 4), c("psD"), O.max)
+                        grp(part, [(c(B, 256 + 2 * (k0 + 4 * h) + j, 512, 32), c(A, a + h, a + 4 * BL, 4), c("G2")) for h in range(4) if k0 + h])
+                else:
+                    for k0 in range(1, 16, 4):
+                        Z, ks, a = bank(), range(k0, min(k0 + 4, 16)), 16 * i0 + BL * k0
+                        lst = []
+                        for k in ks:
+                            o = c(Z, BL * (k - k0), BL * (k - k0 + 1))
+                            lst += [(o, c("NI"), d, True, False)] + ([(o, c("ID"), gv(x0, x0 + BL, k, 16), False, False)] if df and j else [])
+                            lst += [(o, c("ID"), gv(r0, r0 + BL, k, 16), False, True)]
+                        mm(lst)
+                        act(c(A, a, a + BL * len(ks)), c(Z, 0, BL * len(ks)), AF.Abs)
+                        grp(part, [(c(B, 256 + 2 * k + j, 512, 32), c(A, 16 * i0 + BL * k, 16 * i0 + BL * k + BL), G1) for k in ks])
+            grp(part, [(ox, sg, c("N4")), (oy, sg, c("P4"))], True)
+            scan(c("SC2", 2 * i0, 2 * i1), c(B, 256, 512), c("SM2"), 1.0)
+            sc = c("SC2", 2 * i0 + 1, 2 * i1, 2)
+            one([(c(B, 0, 128), sc, c("ID"))])
+            one([(c(B, 128, 256), c("INJ"), sg), (c(B, 128, 256), sc, c("ID"))])
+            act(c("NA", 2 * i0, 2 * i1), c(B, 0, 256), AF.Sign)
+            n = 2 * BW_ if df else BW_
+            oe = c(W, 384, 384 + n)
+            one([(oe, c("ID"), c("BW0", 0, n))] + wrap(oe, "FD" if df else "FY", "NA", 2 * i1 - 16 * n, 2 * i1))
+            OE, XL = c("OE", 2 * w0, 2 * w0 + n), c("XL", 2 * i0, 2 * i0 + 16 * n)
+            vts(OE, oe, 31.0 if df else 1055.0, None, O.add)
+            act(XL, ind(gv(x0 - 1, y0 + BL), OE), AF.Copy)
+            one([(pl, c("HI"), d), (pl, c("QI"), ONE)] + [(pl, c("HI"), c("XL", a, a + BL)) for a in range(2 * i0, 2 * i0 + 16 * n, BL)])
+            vts(c("QB", i0, i1), pl, 8388608.0, 8388608.0, O.add, O.subtract)
+            vtt(EM, NA, c("EZ", i0, i1), O.mult)
+            if not last:
+                z0 = 512 * t + 2 * i0
+                send(to, c("ZE", 2 * i0, 2 * i1), c("Z2", z0, z0 + 2 * BL), 0.8)
+            vtt(ind(LB, c("CU", cu + w0, cu + w1)), ZN, EM, O.add)
+            if last:
+                dma("y", dram(T.yl[:, 4 * i0:4 * i1]), LB, 3.0)
+            else:
+                vtt(ind(c("L2", 1024 * t + 4 * i0, 1024 * t + 4 * i1), c("C2", 16 * t + w0, 16 * t + w1)),
+                    c("Z2", z0, z0 + BL), c("Z2", z0 + BL, z0 + 2 * BL), O.add)
         bias[0] = 0.0
         if not last:
-            mm([(c("psU", 128, 128 + BL), c("R15"), c("ML", b * BL, b * BL + BL), b == 0, b == NB - 1) for b in range(NB)])
-            act(c("JK", 0, BL), c("psU", 128, 128 + BL), AF.Copy, accum=c("AC"))
-        mm([(c("psE", 0, NC), c("HI"), c("OLD"), True, False), (c("psE", 0, NC), c("HI"), c("d"), False, False),
-            (c("psE", 0, NC), c("QI"), c("ON"), False, True)])
-        vts(c("NX"), c("psE", 0, NC), 8388608.0, 8388608.0, O.add, O.subtract)
-        vcopy(ind(c("X"), c("CU", 0, 16)), c("NX"))
+            one([(c("psD", 0, BL), c("R15"), c("SG1", b * BL, b * BL + BL)) for b in range(NB)])
+            act(c("JK"), c("psD", 0, BL), AF.Copy, accum=c("AC"))
         if last:
             dma("y", dram(T.yx[:, :]), c("X"), 4.0)
-        for b in range(NB):
-            i0, i1 = b * BL, (b + 1) * BL
-            vtt(c("EM", i0, i1), c("A2", i0, i1), c("EZ", i0, i1), O.mult)
-            vtt(c("E", i0, i1), c("E", i0, i1), c("EM", i0, i1), O.add)
-            vcopy(ind(c("L", 4 * i0, 4 * i1), c("CU", 16 + i0 // 16, 16 + i1 // 16)), c("E", i0, i1))
-            if last:
-                dma("y", dram(T.yl[:, 4 * i0:4 * i1]), c("L", 4 * i0, 4 * i1), 3.0)
     dma("s", dram(T.yq[:, :]), c("QB"), 2.0)
     return ops
 
 
 def sgs(dur, queue, pred, succ, pri):
     n = len(dur)
-    left, at, fin, qfree, ready, order = [len(p) for p in pred], [0.0] * n, [0.0] * n, {}, {}, []
-    for i in range(n):
-        if not left[i]:
-            ready.setdefault(queue[i], []).append((0.0, i))
-    for _ in range(n):
-        s, q = min((max(qfree.get(q, 0.0), min(lst)[0]), q) for q, lst in ready.items() if lst)
-        _, i, x = max((pri[j], -j, y) for y, j in ready[q] if y <= s + LOOK)
-        i = -i
-        ready[q].remove((x, i))
-        fin[i] = qfree[q] = max(x, qfree.get(q, 0.0)) + dur[i]
-        order.append(i)
+    left, at, fin, gaps, rank = [len(p) for p in pred], [0.0] * n, [0.0] * n, {}, [0] * n
+    ready = [(pri[i], -i) for i in range(n) if not left[i]]
+    for step in range(n):
+        x = max(ready)
+        ready.remove(x)
+        i = -x[1]
+        free = gaps.setdefault(queue[i], [(0.0, 1e9)])
+        j = len(free) - 1
+        while j and free[j - 1][1] > at[i]:
+            j -= 1
+        while free[j][1] - max(free[j][0], at[i]) < dur[i]:
+            j += 1
+        a, b = free[j]
+        s = max(a, at[i])
+        fin[i], rank[i] = s + dur[i], step
+        free[j:j + 1] = [y for y in ((a, s), (fin[i], b)) if y[1] - y[0] > 0.02]
         for k, w in succ[i]:
             left[k] -= 1
             at[k] = max(at[k], fin[i] + w)
             if not left[k]:
-                ready.setdefault(queue[k], []).append((at[k], k))
-    return order, fin
-
-
-def tweak(pri, seed, amp):
-    out = []
-    for i, p in enumerate(pri):
-        h = (i * 2654435761 + seed * 40503 + (i * i + seed) * 97) % 1000003
-        out.append(p + amp * (h / 500001.5 - 1.0) if h % 7 == seed % 7 else p)
-    return out
+                ready.append((pri[k], -k))
+    return sorted(range(n), key=lambda i: (fin[i] - dur[i], rank[i])), fin
 
 
 def schedule(ops):
@@ -421,19 +506,29 @@ def schedule(ops):
             pred[i].append((d, w))
             succ[d].append((i, w))
     for i in range(n - 1, -1, -1):
-        pri[i] = dur[i] + max([pri[k] + w for k, w in succ[i]] or [0.0])
-    pri = [pri[i] + ops[i]["bias"] + NOISE * ((i * 7919 + SEED * 104729 + (i * SEED * 31) % 1013) % 1009) / 1009 for i in range(n)]
-    best = None
-    for _ in range(ROUNDS):
-        order, fin = sgs(dur, queue, pred, succ, pri)
-        end = max(fin[i] + ops[i]["lat"] for i in range(n))
-        if best is None or end < best[0]:
-            best = (end, order, list(pri))
-        _, pri = sgs(dur, queue, succ, pred, fin)
-    order, pri = best[1], best[2]
-    for seed, amp in TWEAKS:
-        pri = tweak(pri, seed, amp)
-    return sgs(dur, queue, pred, succ, pri)[0], pri
+        pri[i] = dur[i] + max([pri[k] + w for k, w in succ[i]] or [ops[i]["lat"]])
+    lat, seed = [o["lat"] for o in ops], [SEED]
+
+    def rnd():
+        seed[0] = (seed[0] * 1103515245 + 12345) % 2147483648
+        return seed[0] / 2147483648
+
+    def forward(p):
+        order, fin = sgs(dur, queue, pred, succ, p)
+        return max(fin[i] + lat[i] for i in range(n)), order, fin
+    cur = best = forward([pri[i] + ops[i]["bias"] for i in range(n)])
+    for r in range(ROUNDS):
+        fin, at, wide, amp, few = cur[2], rnd() * cur[0], (2, 5, 10)[r % 3], (0.5, 1.7, 4.0)[r // 3 % 3], (0.05, 0.2, 0.5)[r // 9 % 3]
+        shift = [amp * (2 * rnd() - 1) if abs(fin[i] - at) < wide and rnd() < few else 0.0 for i in range(n)]
+        if r // 27 % 2:
+            x = forward(sgs(dur, queue, succ, pred, [fin[i] + lat[i] + shift[i] for i in range(n)])[1])
+        else:
+            x = forward([dur[i] - fin[i] + shift[i] for i in range(n)])
+        if x[0] <= cur[0] + 0.1 * (1 - r / ROUNDS) * rnd():
+            cur = x
+        if x[0] < best[0]:
+            best = x
+    return best[1]
 
 
 def emit(g, T, ops, order):
@@ -473,4 +568,6 @@ def rank_program(g, core, T, topo):
     if T.rank_of(core) is None:
         return
     ops = program(g, core, T, topo)
-    emit(g, T, ops, schedule(ops)[0])
+    if not ORDER:
+        ORDER.extend(schedule(ops))
+    emit(g, T, ops, ORDER)

@@ -1,3 +1,4 @@
+import math
 from concourse.mybir import AluOpType as O, ActivationFunctionType as AF
 
 NC, CH, BL, STEPS = 256, 64, 128, 4
@@ -7,24 +8,30 @@ WB = BL * 16 + 32
 f32, bf, i32, u16, f16 = "float32", "bfloat16", "int32", "uint16", "float16"
 SCRATCH = {}
 for _dt, _names in ((bf, "X:4096 PM:%d AD:4096 AX:4096 AY:4096 d:256 SM:1024 SM2:256 QB:256 W1:1 ON:256 G8:32 G2:8 GN:8 F:144 F0:144 NF:144 F8:144 "
-                     "FY:144 FD:144 WF:144 BDa:128 BD:128 NBD:128 ID:128 NI:128 N8:128 HI:128 QI:128 SH:128 P4:128 N4:128 R15:128 ETb:2048 BW0:16 "
+                     "P23:128 N23:128 KW:272 I16:16 MK:256 FD:144 WF:144 BDa:128 BD:128 NBD:128 ID:128 NI:128 N8:128 HI:128 QI:128 SH:128 P4:128 N4:128 R15:128 ETb:2048 BW0:24 F1:144 TR:512 "
                      "TT0:128 TT1:256 OLD:256 NX:256 EQ:256 SC1:256 SC2:512 GE:256 MG:256 XS:256 DS:256 XL:512 AB:512 SG1:256 NA:512 INJ:128 JK:128" % (NB * WB)),
-                    (f32, "L:1024 L2:3072 Z2:1536 COL:16 IO:256 CI:64 B32:32 NR:512 CF:32 A1:16 V2:16 ZD:256 ZE:512 EZ:256 AC:1 TF:6"),
-                    (i32, "D:4112 DO:1024 DI:1024 LI:1024 LJ:1024 EI:256 TH:2 TI:4 PI:2 UI:16 U:16 V3:16 NL:48"),
-                    (u16, "NU:16 BU:256 LU:16 LS:16 PU:256 CU:64 C2:48 DU:32 OF:16 OE:32 GL:16"),
-                    (f16, "F0h:144 F1h:144 ET:2048 LG:256 SG:256 NH:32 PH:256 BH:256 K2:128 IDh:128 HIh:128 HNh:128 TR:512")):
+                    (f32, "L:1024 L2:3072 Z2:1536 COL:16 IO:256 CI:64 B32:32 NR:512 CF:32 A1:16 V2:16 RT:128 ZD:256 ZE:512 EZ:256 AC:1 TF:6"),
+                    (i32, "D:4112 DO:1024 DI:1024 LI:1024 LJ:1024 EI:256 TH:2 TI:4 PI:2 UI:16 U:16 V3:16 NL:48 N2:32"),
+                    (u16, "NU:16 LU:32 LS:16 PU:512 CU:64 C2:48 DU:32 OF:16 OE:32 GL:16"),
+                    (f16, "LG:256 SG:256 NH:32 PH:512")):
     for _x in _names.split():
         SCRATCH[_x.split(":")[0]] = ("sbuf", [128, int(_x.split(":")[1])], _dt)
 SCRATCH["G"] = ("sbuf", [128, NB * GR * 16], bf)
-for _p in ("psU", "psE", "psD", "psB0", "psB1", "psZ0", "psZ1", "psZ2"):
+NK = 4
+for _p in ("psU", "psE", "psB0", "psB1"):
     SCRATCH[_p] = ("psum", [128, 512], f32)
+for _p in range(NK):
+    SCRATCH["psZ%d" % _p] = ("psum", [128, 2048 // NK], f32)
 SEMAPHORES = ["cv", "cs", "ct", "cg"] + ["dma%d" % k for k in range(24)] + ["%s%d" % (x, k) for x in ("ls", "rs") for k in range(17)]
 
-CY, PEC, GA, SC, FX, WAKE, HOP, RISS = 0.00095, 0.0005, 1.5, 3.5, 0.055, 0.06, 2.0, 0.5
-FORM = ("df", "z")
-PART = ("t", "vp")
-BK1, BK2 = ("psD", "psZ2"), ("psZ0", "psZ1")
-STAG, EARLY, ROUNDS, SEED, ORDER = 0.5, 0.0, 4000, 1, []
+CY, PEC, GA, SC, FX, WAKE, HOP, RISS = 0.00095, 0.0005, 1.5, 3.5, 0.05, 0.065, 1.5, 0.5
+DL, PL, SX, PX = 2.2, 1.2, 0.06, 0.005
+CX, CD = (32, 32), (64, 64)
+FORM = ("s", "s")
+YS = ((), ())
+RX, RQ, MS, PUSH = "v", "v", (False, False), "all"
+SPLIT, BK1, BK2 = True, "psZ3", (("psZ0", "psZ1", "psZ2", "psZ3"),) * 2
+CUT, STAG, EARLY, ROUNDS, SEED, ORDER = 2048, 4.0, 0.0, 20000, 1, []
 
 
 def program(g, core, T, topo):
@@ -106,7 +113,7 @@ def program(g, core, T, topo):
             kw["scale"] = scale[0][0] if isinstance(scale, list) else scale
         if accum is not None:
             kw["accum_out"] = accum[0][0]
-        return add("s", cost(out, a, 1.0) + 0.015, out + (accum or []), a + [x for s in (bias, scale) if isinstance(s, list) for x in s],
+        return add("s", cost(out, a, 1.0) + (SX if len(a) == 1 else 0.01), out + (accum or []), a + [x for s in (bias, scale) if isinstance(s, list) for x in s],
                    lambda: g.scalar.activation(out=out[0][0], in_=a[0][0], func=fn, **kw))
 
     def mm(lst, after=()):
@@ -115,10 +122,11 @@ def program(g, core, T, topo):
             for (o, l, r, s, e) in lst:
                 x = g.tensor.matmul(out=o[0][0], lhsT=l[0][0], rhs=r[0][0], start=s, stop=e)
             return x
-        return add("t", 0.03 + sum(max(64, x[2][0][5]) for x in lst) * PEC, [lst[0][0][0]], [v for x in lst for v in x[1] + x[2]], call, after=after)
+        return add("t", PX + sum(max(64, x[2][0][5]) for x in lst) * PEC, [lst[0][0][0]], [v for x in lst for v in x[1] + x[2]], call, after=after, lat=0.03)
 
     def grp(parts, lst, last=False):
-        parts.append(mm([x + (not parts and n == 0, last and n == len(lst) - 1) for n, x in enumerate(lst)], after=parts if last else parts[:1]))
+        if lst:
+            parts.append(mm([x + (not parts and n == 0, last and n == len(lst) - 1) for n, x in enumerate(lst)], after=parts if last else parts[:1]))
 
     def one(lst):
         grp([], lst, True)
@@ -169,39 +177,36 @@ def program(g, core, T, topo):
     bias[0] = 200.0
     vset(c("ON"), 1.0, 0.5)
     vset(c("F"), 0.0, 0.5)
-    vset(c("F0"), 0.0, 0.5)
-    cut = 3072
     asel(c("G8", 0, 8), c("ON", 0, 8), [[-16, 8]], O.is_ge, 0, 1)
     asel(c("G8", 8, 16), c("G8", 0, 8), [[16, 8]], O.is_ge, 15, -1)
-    asel(c("G8", 16, 24), c("ON", 0, 8), [[-16, 8]], O.is_equal, 0, 1)
     G1 = c("G8", 8, 16)
     bias[0] = 100.0
-    vset(c("D", 0, cut), 0.0)
-    iota(c("D", cut, 4112), [[0, 4112 - cut]], 0, 0)
     DROW = [raw(T.D[j:128:16, 0:4096], "D", 0, 4096) for j in range(2)]
     dma("y", c("DO", 0, 256), dram(T.dr[:, :]), 2.2)
     dma("s", c("LI"), dram(T.lg[:, :]), 3.0)
-    dma("y", DROW[0], dram(T.dr[:, :]), 2.5)
     send(reader(0), c("DO", 0, 256), c("DI", 0, 256), 2.0)
     so = send(reader(0), c("LI"), c("LJ"), 3.0)
     vcopy(c("F", 16, 144, 16), G1)
-    vcopy(c("F0", 16, 144, 16), c("G8", 16, 24))
     vts(c("WF"), c("F"), c("W1"), None, O.mult)
-    vcopy(c("F0h"), c("F0"))
+    iota(c("PI", 0, 1), [[0, 1]], 0, 1)
+    iota(c("CI", 48, 64), [[1, 16]], 0, 0)
     bias[0] = 0.0
-    asel(c("G8", 24, 32), c("ON", 0, 8), [[-16, 8]], O.is_equal, -1, 1)
-    vset(c("F1h"), 0.0, 0.5)
-    vcopy(c("F1h", 16, 144, 16), c("G8", 24, 32))
     for k in range(2):
         dma("ys"[k], c("X", 2048 * k, 2048 * k + 2048), dram(T.xr[:, 2048 * k:2048 * k + 2048]), 4.0)
     dma("s", c("EI"), dram(T.e0[:, :]), 4.0)
     dma("y", raw(T.TH[:, :], "TH", 0, 2, True), dram(None), 4.0, [(T.TH[j:128:16, :], T.th[:, :]) for j in range(16)])
-    iota(c("PI", 0, 1), [[0, 1]], 0, 1)
+    for k in range(0, CUT, 512):
+        vset(c("D", k, k + 512), 0.0)
+    for k in range(CUT, 4112, 520):
+        iota(c("D", k, min(k + 520, 4112)), [[0, min(520, 4112 - k)]], 0, 0)
+    dma("y", DROW[0], dram(T.dr[:, :]), 2.5)
+    asel(c("F0"), c("F"), [[-1, 144]], O.is_equal, 16, 1)
+    asel(c("F1"), c("F"), [[-1, 144]], O.is_equal, 15, 1)
     iota(c("CI", 0, 16), [[0, NB], [64, BW_]], 0, 0)
-    iota(c("CI", 16, 32), [[0, NB], [256, BW_]], 0, 0)
-    iota(c("CI", 32, 48), [[-2048, 2], [256, BW_]], 0, 0)
+    iota(c("CI", 16, 32), [[256, 16]], 0, 0)
+    iota(c("CI", 32, 48), [[0, 2], [256, BW_]], 2048, 0)
     iota(c("IO"), [[0, 16], [1, 16]], 0, 0)
-    iota(c("NR", 256, 512), [[4, 256]], 2048, 0)
+    iota(c("TR", 256, 512), [[4, 256]], 0, 0)
     vts(c("PI", 1, 2), c("PI", 0, 1), 15, None, O.bitwise_and)
     K = c("COL", 0, 1)
     vcopy(K, c("PI", 1, 2))
@@ -214,42 +219,35 @@ def program(g, core, T, topo):
     K15 = c("COL", 4, 5)
     act(c("B32", 0, 16), c("CI", 0, 16), AF.Identity, bias=c("COL", 2, 3))
     act(c("B32", 16, 32), c("CI", 16, 32), AF.Identity, bias=c("COL", 1, 2))
-    act(c("BW0"), c("CI", 32, 48), AF.Identity, bias=c("COL", 1, 2))
-    vcopy(c("GL"), c("IO", 0, 16))
-    vts(c("NR", 0, 256), c("IO"), K, 8192.0, O.is_le, O.mult)
-    vts(c("TR", 0, 256), c("NR", 0, 256), 2048.0, None, O.add)
-    vcopy(c("TR", 256, 512), c("NR", 256, 512))
+    act(c("BW0", 0, 8), c("CI", 16, 24), AF.Identity, bias=c("COL", 1, 2))
+    act(c("KW", 256, 272), c("CI", 32, 48), AF.Identity, bias=c("COL", 1, 2))
+    vcopy(c("GL"), c("CI", 48, 64))
+    vts(c("I16"), c("CI", 48, 64), K, None, O.is_equal)
+    vts(c("TR", 0, 256), c("IO"), K, 8192.0, O.is_le, O.mult)
     asel(c("BDa"), c("ON", 0, 128), [[-16, 8], [0, 16]], O.is_ge, 0, 1)
     asel(c("BD"), c("BDa"), [[16, 8], [0, 16]], O.is_ge, 15, -1)
     asel(c("ID"), c("ON", 0, 128), [[-1, 128]], O.is_equal, 0, 1)
     asel(c("BDa"), c("BD"), [[1, 128]], O.is_equal, -1, -1)
-    vset(c("AX", 0, 512), 1.0, 0.5)
-    for k in range(4):
-        asel(c("ETb", 512 * k, 512 * k + 512), c("AX", 0, 512), [[-1, 4], [-16, 8], [0, 16]], O.is_equal, -4 * k, 1, deps=(so,))
-        vcopy(c("ET", 512 * k, 512 * k + 512), c("ETb", 512 * k, 512 * k + 512), k=0.5)
+    for k in range(8):
+        asel(c("ETb", 256 * k, 256 * k + 256), c("ON"), [[-1, 2], [-16, 8], [0, 16]], O.is_equal, -2 * k, 1, deps=(so,))
     act(c("COL", 8, 9), K15, AF.Copy, scale=16.0)
-    act(c("COL", 9, 10), c("COL", 5, 6), AF.Identity, scale=-1025.0 / 16, bias=-1.0)
-    act(c("COL", 10, 11), c("COL", 5, 6), AF.Identity, scale=-4097.0 / 16, bias=-1.0)
+    act(c("COL", 10, 11), c("COL", 5, 6), AF.Identity, scale=2049.0 / 131072, bias=1.0 / 8192)
     asel(c("INJ"), c("BD"), [[1, 128]], O.is_equal, 15, -1)
     for nm, src, v in (("NI", "ID", -1.0), ("N8", "ID", -8192.0), ("HI", "ID", 0.5), ("QI", "ID", -0.25), ("P4", "ID", 4096.0), ("N4", "ID", -4096.0),
                        ("NBD", "BD", -1.0), ("SH", "BDa", 8192.0), ("NF", "F", -1.0), ("F8", "F", 8192.0),
-                       ("FY", "F", c("COL", 9, 10)), ("FD", "F", c("COL", 10, 11))):
+                       ("FD", "F", c("COL", 10, 11))) + ((("P23", "ID", 8388608.0), ("N23", "ID", -8388608.0)) if "t" in RX + RQ else ()):
         act(c(nm), c(src), AF.Copy, scale=v)
     act(c("G2"), G1, AF.Copy, scale=2.0)
     act(c("GN"), G1, AF.Copy, scale=-1.0)
     act(c("R15"), c("ON", 0, 128), AF.Copy, scale=c("COL", 8, 9))
-    vcopy(c("IDh"), c("ID"), k=0.5)
-    vts(c("HIh"), c("ID"), 0.5, None, O.mult, k=0.5)
-    vts(c("HNh"), c("ID"), -0.5, None, O.mult, k=0.5)
-    vts(c("K2"), c("ON", 0, 128), 2048.0, None, O.mult, k=0.5)
-    vset(c("SM"), 1.0, 0.5)
-    vset(c("SM", 15, 1024, 16), 0.0)
-    vset(c("SM2"), 1.0, 0.5)
-    vset(c("SM2", 1, 256, 32), 0.0)
+    act(c("KW", 0, 256), c("ON"), AF.Copy, scale=-10240.0)
+    for k in range(4):
+        asel(c("SM", 256 * k, 256 * k + 256), c("ON"), [[0, 16], [1, 16]], O.not_equal, -15, 0, deps=(so,))
+    asel(c("SM2"), c("ON"), [[0, 8], [1, 32]], O.not_equal, -1, 0, deps=(so,))
     for b in range(NB):
-        vset(c("PM", b * WB + 16, b * WB + 32), 0.0, 0.5)
-        vset(gv(b * GR, b * GR + 1), 0.0, 0.5)
-    vcopy(c("L"), c("LI"))
+        act(c("PM", b * WB + 16, b * WB + 32), c("ON", 0, 16), AF.Copy, scale=0.0)
+        act(gv(b * GR, b * GR + 1), c("ON", 0, 16), AF.Copy, scale=0.0)
+    asel(c("L"), c("LI"), [[0, 1024]], O.is_ge, 0, 0, deps=(so,))
     vts(c("TI", 0, 2), c("TH"), 4, None, O.arith_shift_right)
     vts(c("TI", 2, 4), c("TH"), 15, None, O.bitwise_and)
     vts(c("TF", 0, 2), c("TI", 0, 2), c("COL", 5, 6), None, O.mult)
@@ -267,94 +265,117 @@ def program(g, core, T, topo):
     def wrap(out, name, v, lo, hi):
         return [(out, sel(name, m), c(v, lo + m, hi, 16)) for m in range(16)]
 
+    def half(out, ps, terms, how):
+        one([(ps, c("QI"), ONE)] + [(ps, c("HI"), x) for x in terms] + ([(ps, c("P23"), ONE), (ps, c("N23"), ONE)] if how == "t" else []))
+
+        def rest():
+            if how == "v":
+                vts(out, ps, 8388608.0, 8388608.0, O.add, O.subtract)
+            elif how == "t":
+                act(out, ps, AF.Copy)
+            else:
+                act(c("RT"), ps, AF.Identity, bias=8388608.0)
+                act(out, c("RT"), AF.Identity, bias=-8388608.0)
+        return rest
+
     rot = [0]
 
-    def bank(names=("psZ0", "psZ1", "psZ2")):
+    def bank(names):
         rot[0] += 1
         return names[rot[0] % len(names)]
 
     for t in range(STEPS):
         to, last = reader(t + 1), t == STEPS - 1
-        NU = c("NU")
         cu, cv = 32 * (t % 2), 32 * ((t + 1) % 2)
         LT, L2 = (c("L"), c("L2", 1024 * (t - 1), 1024 * t)) if t else (c("LI"), c("LJ"))
-        if not last:
+        if not last and PUSH == "new":
             send(to, c("L"), c("L2", 1024 * t, 1024 * t + 1024), 3.0)
-        one(wrap(c("psU", 0, 16), "WF", "QB", 0, NC))
-        vcopy(c("UI"), c("psU", 0, 16))
-        vts(c("U"), c("UI"), 4095, None, O.bitwise_and)
-        vts(c("A1"), c("U"), 592.0, None, O.add)
-        vtt(c("V2"), c("A1"), c("A1"), O.mult)
-        if t:
-            vts(c("V3"), c("V2"), c("AC"), 75520.0, O.add, O.add)
-        else:
-            vts(c("V3"), c("V2"), 42752.0, None, O.add)
         N = c("NL", 0, 16)
-        vts(N, c("V3"), 5, 4095, O.arith_shift_right, O.bitwise_and)
-        vcopy(NU, N)
-        vcopy(c("LG"), ind(c("D", 0, 4096), NU))
-        one(wrap(c("psU", 32, 48), "F0h", "LG", 0, NC))
-        vcopy(c("LU"), c("psU", 32, 48))
-        vcopy(c("PU"), ind(LT, c("LU")))
-        if t == 0:
-            dma("y", DROW[1], c("DI", 0, 256), 2.5)
-            vcopy(c("SG"), ind(c("D", 0, 4096), NU))
-        one(wrap(c("psE", 0, 16), "F1h", "LG" if t else "SG", 0, NC))
-        vcopy(c("LS"), c("psE", 0, 16))
-        vcopy(c("BU"), ind(L2, c("LS")))
+        for i0, i1, W, W2 in ((0, BL, "psU", "psU"), (BL, NC, "psE", "psE")) if t and SPLIT else ((0, NC, "psU", "psE"),):
+            w0, w1 = i0 // 16, i1 // 16
+            UI, U, A1, V2, V3, NL, NU, LU, LS = [c(x, w0, w1) for x in ("UI", "U", "A1", "V2", "V3", "NL", "NU", "LU", "LS")]
+            bias[0] = STAG * (i0 == 0)
+            one(wrap(c(W, w0, w1), "WF", "QB", i0, i1))
+            vcopy(UI, c(W, w0, w1))
+            vts(U, UI, 4095, None, O.bitwise_and)
+            vts(A1, U, 592.0, None, O.add)
+            vtt(V2, A1, A1, O.mult)
+            if t:
+                vts(V3, V2, c("AC"), 75520.0, O.add, O.add)
+            else:
+                vts(V3, V2, 42752.0, None, O.add)
+            vts(NL, V3, 5, 4095, O.arith_shift_right, O.bitwise_and)
+            if t:
+                vcopy(NU, NL)
+            if t:
+                vcopy(c("LG", i0, i1), ind(c("D", 0, 4096), NU))
+            else:
+                vts(c("N2", 0, 16), NL, 8, None, O.arith_shift_right)
+                vts(c("N2", 16, 32), NL, 255, None, O.bitwise_and)
+                vcopy(c("DU"), c("N2"))
+                act(c("MK"), ind(c("I16"), c("DU", 0, 16)), AF.Copy)
+                vtt(c("LG"), ind(c("DO", 0, 256), c("DU", 16, 32)), c("MK"), O.mult)
+                vtt(c("SG"), ind(c("DI", 0, 256), c("DU", 16, 32)), c("MK"), O.mult)
+            if t and SPLIT:
+                LU, LS = c("LU", 2 * w0, 2 * w0 + BW_), c("LU", 2 * w0 + BW_, 2 * w1)
+                one(wrap(c(W, 32, 40), "F0", "LG", i0, i1))
+                one(wrap(c(W, 40, 48), "F1", "LG", i0, i1))
+                vcopy(c("LU", 2 * w0, 2 * w1), c(W, 32, 48))
+                vcopy(c("PU", i0, i1), ind(LT, LU))
+                vcopy(c("PU", NC + i0, NC + i1), ind(L2, LS))
+                continue
+            one(wrap(c(W, 32 + w0, 32 + w1), "F0" if t else "F", "LG", i0, i1))
+            vcopy(LU, c(W, 32 + w0, 32 + w1))
+            vcopy(c("PU", i0, i1), ind(LT, LU))
+            one(wrap(c(W2, w0, w1), "F1" if t else "F", "LG" if t else "SG", i0, i1))
+            vcopy(LS, c(W2, w0, w1))
+            vcopy(c("PU", NC + i0, NC + i1), ind(L2, LS))
+        bias[0] = 0.0
         for a in range(0, NC, CH):
             r0 = a // BL * GR + 1 + a % BL
-            act(gv(r0, r0 + CH), ind(c("X"), c("PU", a, a + CH)), AF.Copy)
+            for h in range(0, CH, CX[a // BL]):
+                act(gv(r0 + h, r0 + h + CX[a // BL]), ind(c("X"), c("PU", a + h, a + h + CX[a // BL])), AF.Copy)
             y0 = a // BL * WB + 17 + 16 * (a % BL)
             scan(c("PM", y0, y0 + 16 * CH), gv(r0, r0 + CH), c("SM", 0, 16 * CH), 0.5)
         vts(c("PH"), c("PU"), -2048.0, None, O.add, k=0.5)
-        vts(c("BH"), c("BU"), -2048.0, None, O.add, k=0.5)
         vts(c("NL", 16, 32), c("UI"), 3, None, O.bitwise_and)
         vts(c("NL", 32, 48), c("UI"), 15, None, O.bitwise_and)
         vtt(c("CF"), c("NL", 16, 48), c("B32"), O.add)
         vcopy(c("CU", cu, cu + 32), c("CF"))
-        for a in range(0, NC, BL):
-            act(c("OLD", a, a + BL), ind(c("X", 16 * a, 16 * a + 16 * BL), c("CU", cu + 16 + a // 16, cu + 16 + a // 16 + BW_)), AF.Copy)
+        act(c("OLD"), ind(c("X"), c("CU", cu + 16, cu + 32)), AF.Copy)
         if not last:
             bias[0] = EARLY
-            send(to, c("CU", cu, cu + 16), c("C2", 16 * t, 16 * t + 16))
+            if PUSH == "new":
+                send(to, c("CU", cu, cu + 16), c("C2", 16 * t, 16 * t + 16))
             vts(c("NH"), c("NL", 0, 32), -2048.0, None, O.add)
-            one([(c("psE"), c("IDh"), c("TR"))] + [(c("psE", m, 512, 16), c("ET", 128 * m, 128 * m + 128), c("NH")) for m in range(16)])
-            act(c("NR"), c("psE"), AF.Copy)
+            one([(c(BK1, 0, 512), c("ID"), c("TR"))] + [(c(BK1, m, 512, 16), c("ETb", 128 * m, 128 * m + 128), c("NH")) for m in range(16)])
+            act(c("NR"), c(BK1, 0, 512), AF.Identity, bias=2048.0)
             vtt(c("EQ"), ind(N, c("GL")), c("NR", 0, 256), O.is_equal)
-            one([(c("psE", 0, 16), c("IDh"), c("NH", 0, 16))] + wrap(c("psE", 0, 16), "F8", "EQ", 0, NC))
-            vts(c("DU", 0, 32, 2), c("psE", 0, 16), c("COL", 3, 4), 2048.0, O.min, O.add)
+            one([(c(BK1, 0, 16), c("ID"), c("NH", 0, 16))] + wrap(c(BK1, 0, 16), "F8", "EQ", 0, NC))
+            vts(c("DU", 0, 32, 2), c(BK1, 0, 16), c("COL", 3, 4), 2048.0, O.min, O.add)
             for n in range(15, -1, -1):
                 vcopy(ind(c("D"), c("DU", 2 * n, 2 * n + 1)), c("NR", 256 + 16 * n, 272 + 16 * n))
             DO, DI = [c(x, 256 * t + 256, 256 * t + 512) for x in ("DO", "DI")]
-            dma("y", DO, DROW[0], 2.5)
-            send(to, DO, DI, 0.8)
-            dma("y", DROW[1], DI, 2.5)
+            dma("y", DO, DROW[0], DL)
+            send(to, DO, DI, DL - 1.5)
+            dma("y", DROW[1], DI, DL)
         for b in range(NB):
             i0, i1, w0, w1, x0 = b * BL, (b + 1) * BL, b * BW_, (b + 1) * BW_, b * GR + 1
-            y0, df, B = x0 + BL, FORM[b] == "df", ("psU", "psE")[b]
+            y0, B = x0 + BL, ("psU", "psE")[b]
             bias[0] = STAG * (NB - 1 - b)
             part = []
             grp(part, [(c(B, 0, 128), ONE, c("TT0"))])
             for a in range(0, BL, CH):
-                names = ind(c("X"), c("BU", i0 + a, i0 + a + CH))
-                if df:
-                    vtt(gv(y0 + a, y0 + a + CH), names, gv(x0 + a, x0 + a + CH), O.subtract)
-                    vts(c("AD", 16 * (i0 + a), 16 * (i0 + a + CH)), gv(y0 + a, y0 + a + CH), 0.0, None, O.max, k=0.5)
+                for h in range(a, a + CH, CD[b]):
+                    names = ind(c("X"), c("PU", NC + i0 + h, NC + i0 + h + CD[b]))
+                    vtt(gv(y0 + h, y0 + h + CD[b]), names, gv(x0 + h, x0 + h + CD[b]), O.subtract)
+                if FORM[b] == "s":
+                    act(c("AD", 16 * (i0 + a), 16 * (i0 + a + CH)), gv(y0 + a, y0 + a + CH), AF.Abs)
                 else:
-                    act(gv(y0 + a, y0 + a + CH), names, AF.Copy)
-                    for h in range(a, a + CH, 32):
-                        Z, dif = c(bank(BK1)), []
-                        if FORM[b] == "z":
-                            one([(Z, c("ID"), gv(x0 + h, x0 + h + 32))])
-                            vtt(c("AD", 16 * (i0 + h), 16 * (i0 + h + 32)), gv(y0 + h, y0 + h + 32), Z, O.max)
-                            continue
-                        grp(dif, [(Z, c("NI"), gv(x0 + h, x0 + h + 32))])
-                        grp(dif, [(Z, c("ID"), gv(y0 + h, y0 + h + 32))], True)
-                        act(c("AD", 16 * (i0 + h), 16 * (i0 + h + 32)), Z, AF.Abs)
-            for r0 in {"df": (y0,), "y": (), "z": (x0, y0)}[FORM[b]]:
-                grp(part, [(c(B, k, 128, 16), gv(r0, r0 + BL, k, 16), c("GN")) for k in range(15)])
-            grp(part, [(c(B, k, 128, 16), c("AD", 16 * i0 + k, 16 * i1, 16), G1 if FORM[b] == "y" else c("G2")) for k in range(15)], True)
+                    vts(c("AD", 16 * (i0 + a), 16 * (i0 + a + CH)), gv(y0 + a, y0 + a + CH), 0.0, None, O.max, k=0.5)
+            if FORM[b] == "v":
+                grp(part, [(c(B, k, 128, 16), gv(y0, y0 + BL, k, 16), c("GN")) for k in range(15)])
+            grp(part, [(c(B, k, 128, 16), c("AD", 16 * i0 + k, 16 * i1, 16), G1 if FORM[b] == "s" else c("G2")) for k in range(15)], True)
             GE = c("GE", i0, i1)
             scan(c("SC1", i0, i1), c(B, 0, 128), c("SM", 0, 128), 1.0)
             one([(c(B, 128, 256), c("SC1", i0, i1), c("ID"))])
@@ -362,108 +383,90 @@ def program(g, core, T, topo):
             one([(c(B, 0, BW_), c("ID"), c("BW0", 0, BW_))] + wrap(c(B, 0, BW_), "NF", "GE", i0, i1))
             OF = c("OF", w0, w1)
             vts(OF, c(B, 0, BW_), 16.0, None, O.add)
-            vtt(c("MG", i0, i1), ind(c("PM", b * WB + 16, b * WB + 16 + 16 * BL), OF), c("QB", i0, i1), O.subtract)
-            act(c("d", i0, i1), c("MG", i0, i1), AF.Abs)
+            M = ind(c("PM", b * WB + 16, b * WB + 16 + 16 * BL), OF)
+            if MS[b]:
+                act(c("MG", i0, i1), M, AF.Copy)
+                one([(c(B, 0, BL), c("NI"), c("QB", i0, i1)), (c(B, 0, BL), c("ID"), c("MG", i0, i1))])
+                act(c("d", i0, i1), c(B, 0, BL), AF.Abs)
+            else:
+                vtt(c("MG", i0, i1), M, c("QB", i0, i1), O.subtract)
+                act(c("d", i0, i1), c("MG", i0, i1), AF.Abs)
         for b in range(NB):
             i0, i1, w0, w1, x0 = b * BL, (b + 1) * BL, b * BW_, (b + 1) * BW_, b * GR + 1
-            y0, df, B, W = x0 + BL, FORM[b] == "df", "psB%d" % b, ("psU", "psE")[b]
+            y0, B, W = x0 + BL, "psB%d" % b, ("psU", "psE")[b]
             bias[0] = STAG * (NB - 1 - b)
             d, xs, ds, sg, GE, OF, NA = [c(x, i0, i1) for x in ("d", "XS", "DS", "SG1", "GE")] + [c("OF", w0, w1), c("NA", 2 * i0, 2 * i0 + BL)]
             act(xs, ind(gv(x0, x0 + BL), OF), AF.Copy)
             act(ds, ind(gv(y0, y0 + BL), OF), AF.Copy)
             px, py, pl = c(W, 0, BL), c(W, BL, 2 * BL), c(W, 2 * BL, 3 * BL)
             one([(px, c("ID"), xs), (px, c("NI"), d)])
-            one([(py, c("ID"), ds), (py, c("NI"), d)] + ([(py, c("ID"), xs)] if df else []))
-            nx = c(W, 3 * BL, 4 * BL)
-            one([(nx, c("HI"), c("OLD", i0, i1)), (nx, c("HI"), d), (nx, c("QI"), ONE)])
+            one([(py, c("ID"), ds), (py, c("NI"), d), (py, c("ID"), xs)])
+            nx = half(c("NX", i0, i1), c(W, 3 * BL, 4 * BL), [c("OLD", i0, i1), d], RX)
             act(c("AB", 2 * i0, 2 * i1), c(W, 0, 2 * BL), AF.Abs)
+            if RX != "v":
+                nx()
             one([(pl, c("NBD"), c("AB", 2 * i0, 2 * i0 + BL)), (pl, c("N8"), GE), (pl, c("BD"), c("AB", 2 * i0 + BL, 2 * i1))])
-            one([(px, c("HIh"), c("BH", i0, i1)), (px, c("HNh"), c("PH", i0, i1))])
-            one([(py, c("HIh"), c("BH", i0, i1)), (py, c("HIh"), c("PH", i0, i1)), (py, c("IDh"), c("K2"))])
             act(sg, pl, AF.Sign, bias=-8192.5, scale=-1.0)
-            ZN, EM = c("ZE", 2 * i0, 2 * i0 + BL), c("ZE", 2 * i0 + BL, 2 * i1)
-            vtt(c("ZD", i0, i1), px, sg, O.mult)
-            vtt(ZN, py, c("ZD", i0, i1), O.add)
-            vts(c("NX", i0, i1), nx, 8388608.0, 8388608.0, O.add, O.subtract)
-            vcopy(ind(c("X", 16 * i0, 16 * i1), c("CU", cu + 16 + w0, cu + 16 + w1)), c("NX", i0, i1))
-            LB = c("L", 4 * i0, 4 * i1)
-            old = ind(LB, c("CU", cv + w0, cv + w1)) if t else c("EI", i0, i1)
-            vtt(c("EZ", i0, i1), old, ZN, O.subtract)
+            if b == NB - 1 and not last:
+                one([(pl, c("R15"), c("SG1", a, a + BL)) for a in range(0, NC, BL)])
+                act(c("JK"), pl, AF.Copy, accum=c("AC"))
+            if RX == "v":
+                nx()
+            vcopy(ind(c("X"), c("CU", cu + 16 + w0, cu + 16 + w1)), c("NX", i0, i1))
             part, ox, oy = [], c(B, 256, 512, 2), c(B, 257, 512, 2)
             grp(part, [(c(B, 256, 512), ONE, c("TT1"))])
             grp(part, [(ox, GE, c("SH")), (oy, GE, c("SH"))])
-            if "v" in PART[b]:
-                mm([(c("psD", j, 512, 4), c("ID"), d, True, True) for j in range(4)])
-            if PART[b] in "tu":
-                for o in (256, 257) if PART[b] == "u" else (257,):
-                    grp(part, [(c(B, o + 2 * k, 512, 32), gv(x0, x0 + BL, k, 16), G1) for k in range(1, 16)])
-                    grp(part, [(c(B, o, 512, 2), d, c("NBD"))])
-                grp(part, [(c(B, 257 + 2 * k, 512, 32), gv(y0, y0 + BL, k, 16), c("GN")) for k in range(1, 16)])
-                for k0 in range(4):
-                    Z, a, dif = bank(BK2), 16 * i0 + 4 * BL * k0, []
-                    grp(dif, [(c(Z), c("NI"), gv(x0, x0 + BL, k0, 4))])
-                    grp(dif, [(c(Z, j, 512, 4), c("ID"), d) for j in range(4)], True)
-                    if PART[b] == "u":
-                        vts(c("AX", a, a + 4 * BL), c(Z), 0.0, None, O.max)
-                    else:
-                        act(c("AX", a, a + 4 * BL), c(Z), AF.Abs)
-                    vtt(c("AY", a, a + 4 * BL), gv(y0, y0 + BL, k0, 4), c(Z), O.max)
-                    for j, (A, S) in enumerate((("AX", G1 if PART[b] == "t" else c("G2")), ("AY", c("G2")))):
-                        grp(part, [(c(B, 256 + 2 * (k0 + 4 * h) + j, 512, 32), c(A, a + h, a + 4 * BL, 4), S) for h in range(4) if k0 + h])
-            for j, (r0, A) in enumerate(((x0, "AX"), (y0, "AY")) if PART[b] not in "tu" else ()):
-                if PART[b][j] == "p":
-                    for k0 in range(4):
-                        Z, a, dif = bank(), 16 * i0 + 4 * BL * k0, []
-                        grp(dif, [(c(Z), c("ID"), gv(r, r + BL, k0, 4)) for r in ((x0, y0) if df and j else (r0,))])
-                        grp(dif, [(c(Z, h, 512, 4), c("NI"), d) for h in range(4)], True)
-                        act(c(A, a, a + 4 * BL), c(Z), AF.Abs)
-                        grp(part, [(c(B, 256 + 2 * (k0 + 4 * h) + j, 512, 32), c(A, a + h, a + 4 * BL, 4), G1) for h in range(4) if k0 + h])
-                elif PART[b][j] == "v":
-                    grp(part, [(c(B, 256 + 2 * k + j, 512, 32), gv(r0, r0 + BL, k, 16), c("GN")) for k in range(1, 16)])
-                    grp(part, [(c(B, 256 + j, 512, 2), d, c("NBD"))])
-                    for k0 in range(4):
-                        a = 16 * i0 + 4 * BL * k0
-                        vtt(c(A, a, a + 4 * BL), gv(r0, r0 + BL, k0, 4), c("psD"), O.max)
-                        grp(part, [(c(B, 256 + 2 * (k0 + 4 * h) + j, 512, 32), c(A, a + h, a + 4 * BL, 4), c("G2")) for h in range(4) if k0 + h])
+            ks = [k for k in range(1, 16) if k % NK not in YS[b]]
+            for r0, S in ((x0, G1), (y0, c("GN"))):
+                grp(part, [(c(B, 257 + 2 * k, 512, 32), gv(r0, r0 + BL, k, 16), S) for k in ks])
+            grp(part, [(c(B, 257 + 2 * k0, 512, 2 * NK), d, c("NBD", k0, 128, NK)) for k0 in range(NK) if k0 not in YS[b]] if YS[b] else [(oy, d, c("NBD"))])
+            KS, CB = 16 // NK, 32 * NK
+            for k0 in range(NK):
+                Z, a, dif = bank(BK2[b]), 16 * i0 + KS * BL * k0, [[] for _ in range(0, BL, CB)]
+                for h in range(0, BL, CB):
+                    grp(dif[h // CB], [(c(Z, KS * h, KS * h + 512), c("NI"), gv(x0 + h, x0 + h + CB, k0, NK))])
+                for h in range(0, BL, CB):
+                    grp(dif[h // CB], [(c(Z, KS * h + j, KS * h + 512, KS), c("ID"), c("d", i0 + h, i0 + h + CB)) for j in range(KS)], k0 not in YS[b])
+                act(c("AX", a, a + KS * BL), c(Z), AF.Abs)
+                if k0 in YS[b]:
+                    for h in range(0, BL, CB):
+                        grp(dif[h // CB], [(c(Z, KS * h, KS * h + 512), c("NI"), gv(y0 + h, y0 + h + CB, k0, NK))], True)
+                    act(c("AY", a, a + KS * BL), c(Z), AF.Abs)
                 else:
-                    for k0 in range(1, 16, 4):
-                        Z, ks, a = bank(), range(k0, min(k0 + 4, 16)), 16 * i0 + BL * k0
-                        lst = []
-                        for k in ks:
-                            o = c(Z, BL * (k - k0), BL * (k - k0 + 1))
-                            lst += [(o, c("NI"), d, True, False)] + ([(o, c("ID"), gv(x0, x0 + BL, k, 16), False, False)] if df and j else [])
-                            lst += [(o, c("ID"), gv(r0, r0 + BL, k, 16), False, True)]
-                        mm(lst)
-                        act(c(A, a, a + BL * len(ks)), c(Z, 0, BL * len(ks)), AF.Abs)
-                        grp(part, [(c(B, 256 + 2 * k + j, 512, 32), c(A, 16 * i0 + BL * k, 16 * i0 + BL * k + BL), G1) for k in ks])
+                    vtt(c("AY", a, a + KS * BL), gv(y0, y0 + BL, k0, NK), c(Z), O.max)
+                for j, (A, S) in enumerate((("AX", G1), ("AY", G1 if k0 in YS[b] else c("G2")))):
+                    grp(part, [(c(B, 256 + 2 * (k0 + NK * h) + j, 512, 32), c(A, a + h, a + KS * BL, KS), S) for h in range(KS) if k0 + h])
             grp(part, [(ox, sg, c("N4")), (oy, sg, c("P4"))], True)
             scan(c("SC2", 2 * i0, 2 * i1), c(B, 256, 512), c("SM2"), 1.0)
             sc = c("SC2", 2 * i0 + 1, 2 * i1, 2)
             one([(c(B, 0, 128), sc, c("ID"))])
             one([(c(B, 128, 256), c("INJ"), sg), (c(B, 128, 256), sc, c("ID"))])
-            act(c("NA", 2 * i0, 2 * i1), c(B, 0, 256), AF.Sign)
-            n = 2 * BW_ if df else BW_
-            oe = c(W, 384, 384 + n)
-            one([(oe, c("ID"), c("BW0", 0, n))] + wrap(oe, "FD" if df else "FY", "NA", 2 * i1 - 16 * n, 2 * i1))
-            OE, XL = c("OE", 2 * w0, 2 * w0 + n), c("XL", 2 * i0, 2 * i0 + 16 * n)
-            vts(OE, oe, 31.0 if df else 1055.0, None, O.add)
-            act(XL, ind(gv(x0 - 1, y0 + BL), OE), AF.Copy)
-            one([(pl, c("HI"), d), (pl, c("QI"), ONE)] + [(pl, c("HI"), c("XL", a, a + BL)) for a in range(2 * i0, 2 * i0 + 16 * n, BL)])
-            vts(c("QB", i0, i1), pl, 8388608.0, 8388608.0, O.add, O.subtract)
-            vtt(EM, NA, c("EZ", i0, i1), O.mult)
-            if not last:
+            act(c("NA", 2 * i0, 2 * i1), c(B, 0, 256), AF.Relu, scale=-16384.0, bias=8192.0)
+            ZN, EM = c("ZE", 2 * i0, 2 * i0 + BL), c("ZE", 2 * i0 + BL, 2 * i1)
+            oe, OE, part = c(B, 2 * BL, 2 * BL + 2 * BW_), c("OE", 2 * w0, 2 * w1), []
+            grp(part, [(c(W, 0, 2 * BL), c("ID"), c("KW", 0, 256)), (px, c("ID"), c("PH", i0, i1)), (px, c("N4"), sg),
+                       (py, c("ID"), c("PH", NC + i0, NC + i1)), (py, c("P4"), sg)])
+            grp(part, [(px, c("ID"), NA), (py, c("ID"), NA)], True)
+            one([(oe, c("ID"), c("KW", 256, 272))] + wrap(oe, "FD", "NA", 2 * i0, 2 * i1))
+            vts(OE, oe, 16.0, None, O.add)
+            act(c("ZD", i0, i1), px, AF.Copy)
+            vtt(ZN, py, c("ZD", i0, i1), O.max)
+            act(c("XL", 2 * i0, 2 * i1), ind(gv(x0 - 1, y0 + BL), OE), AF.Copy)
+            half(c("QB", i0, i1), pl, [d] + [c("XL", a, a + BL) for a in (2 * i0, 2 * i0 + BL)], RQ)()
+            LB = c("L", 4 * i0, 4 * i1)
+            vtt(EM, ind(LB, c("CU", cv + w0, cv + w1)) if t else c("EI", i0, i1), NA, O.subtract)
+            if not last and PUSH == "new":
                 z0 = 512 * t + 2 * i0
                 send(to, c("ZE", 2 * i0, 2 * i1), c("Z2", z0, z0 + 2 * BL), 0.8)
-            vtt(ind(LB, c("CU", cu + w0, cu + w1)), ZN, EM, O.add)
+            vtt(ind(LB, c("CU", cu + w0, cu + w1)), ZN, EM, O.max)
             if last:
                 dma("y", dram(T.yl[:, 4 * i0:4 * i1]), LB, 3.0)
-            else:
+            elif PUSH == "new":
                 vtt(ind(c("L2", 1024 * t + 4 * i0, 1024 * t + 4 * i1), c("C2", 16 * t + w0, 16 * t + w1)),
-                    c("Z2", z0, z0 + BL), c("Z2", z0 + BL, z0 + 2 * BL), O.add)
+                    c("Z2", z0, z0 + BL), c("Z2", z0 + BL, z0 + 2 * BL), O.max)
+            else:
+                send(to, LB, c("L2", 1024 * t + 4 * i0, 1024 * t + 4 * i1), PL)
         bias[0] = 0.0
-        if not last:
-            one([(c("psD", 0, BL), c("R15"), c("SG1", b * BL, b * BL + BL)) for b in range(NB)])
-            act(c("JK"), c("psD", 0, BL), AF.Copy, accum=c("AC"))
         if last:
             dma("y", dram(T.yx[:, :]), c("X"), 4.0)
     dma("s", dram(T.yq[:, :]), c("QB"), 2.0)
@@ -472,28 +475,38 @@ def program(g, core, T, topo):
 
 def sgs(dur, queue, pred, succ, pri):
     n = len(dur)
-    left, at, fin, gaps, rank = [len(p) for p in pred], [0.0] * n, [0.0] * n, {}, [0] * n
+    left, at, fin, gaps, placed = [len(p) for p in pred], [0.0] * n, [0.0] * n, {q: [(0.0, 1e9)] for q in set(queue)}, []
     ready = [(pri[i], -i) for i in range(n) if not left[i]]
-    for step in range(n):
+    while ready:
         x = max(ready)
         ready.remove(x)
         i = -x[1]
-        free = gaps.setdefault(queue[i], [(0.0, 1e9)])
+        free, s, d = gaps[queue[i]], at[i], dur[i]
         j = len(free) - 1
-        while j and free[j - 1][1] > at[i]:
+        while j and free[j - 1][1] > s:
             j -= 1
-        while free[j][1] - max(free[j][0], at[i]) < dur[i]:
-            j += 1
         a, b = free[j]
-        s = max(a, at[i])
-        fin[i], rank[i] = s + dur[i], step
-        free[j:j + 1] = [y for y in ((a, s), (fin[i], b)) if y[1] - y[0] > 0.02]
+        while b - (a if a > s else s) < d:
+            j += 1
+            a, b = free[j]
+        if a > s:
+            s = a
+        f = fin[i] = s + d
+        placed.append((s, len(placed), i))
+        if s - a > 0.02:
+            free[j:j + 1] = [(a, s), (f, b)] if b - f > 0.02 else [(a, s)]
+        elif b - f > 0.02:
+            free[j] = (f, b)
+        else:
+            del free[j]
         for k, w in succ[i]:
             left[k] -= 1
-            at[k] = max(at[k], fin[i] + w)
+            if at[k] < f + w:
+                at[k] = f + w
             if not left[k]:
                 ready.append((pri[k], -k))
-    return sorted(range(n), key=lambda i: (fin[i] - dur[i], rank[i])), fin
+    placed.sort()
+    return [x[2] for x in placed], fin
 
 
 def schedule(ops):
@@ -502,7 +515,7 @@ def schedule(ops):
     pred, succ, pri = [[] for _ in ops], [[] for _ in ops], [0.0] * n
     for i, o in enumerate(ops):
         for d in o["hard"] + o["soft"]:
-            w = 0.0 if d in o["soft"] else ops[d]["lat"] + (WAKE if ops[d]["q"] != o["q"] else 0.03)
+            w = 0.0 if d in o["soft"] else ops[d]["lat"] + WAKE
             pred[i].append((d, w))
             succ[d].append((i, w))
     for i in range(n - 1, -1, -1):
@@ -516,16 +529,45 @@ def schedule(ops):
     def forward(p):
         order, fin = sgs(dur, queue, pred, succ, p)
         return max(fin[i] + lat[i] for i in range(n)), order, fin
+    def waits(x):
+        fin, before, tail, out = x[2], [-1] * n, {}, []
+        for i in x[1]:
+            before[i] = tail.get(queue[i], -1)
+            tail[queue[i]] = i
+        i = max(range(n), key=lambda j: fin[j] + lat[j])
+        while True:
+            s = fin[i] - dur[i]
+            k = max([p for p, w in pred[i] if fin[p] + w > s - 1e-6] or [-1])
+            if k < 0:
+                k = before[i]
+                if k < 0 or fin[k] < s - 0.021:
+                    return out
+                out.append((k, i))
+            i = k
     cur = best = forward([pri[i] + ops[i]["bias"] for i in range(n)])
+    pairs = waits(cur)
     for r in range(ROUNDS):
-        fin, at, wide, amp, few = cur[2], rnd() * cur[0], (2, 5, 10)[r % 3], (0.5, 1.7, 4.0)[r // 3 % 3], (0.05, 0.2, 0.5)[r // 9 % 3]
-        shift = [amp * (2 * rnd() - 1) if abs(fin[i] - at) < wide and rnd() < few else 0.0 for i in range(n)]
-        if r // 27 % 2:
-            x = forward(sgs(dur, queue, succ, pred, [fin[i] + lat[i] + shift[i] for i in range(n)])[1])
+        fin = cur[2]
+        if r % 4 and pairs:
+            p = [dur[i] - fin[i] for i in range(n)]
+            for _ in range(1 + r // 4 % 3):
+                (u, v), d = pairs[int(rnd() * len(pairs))], (0.01, 0.3, 1.0, 2.0)[int(rnd() * 4)]
+                if rnd() < 0.5:
+                    todo, top = [v], p[u] + d
+                    while todo:
+                        a = todo.pop()
+                        if p[a] < top:
+                            p[a] = top + 1e-4 * rnd()
+                            todo.extend(b for b, w in pred[a])
+                else:
+                    p[u] = p[v] - d
+            x = forward(p)
         else:
-            x = forward([dur[i] - fin[i] + shift[i] for i in range(n)])
-        if x[0] <= cur[0] + 0.1 * (1 - r / ROUNDS) * rnd():
-            cur = x
+            at, wide, amp, few = rnd() * cur[0], (2, 5, 10)[r // 4 % 3], (0.5, 1.7, 4.0)[r // 12 % 3], (0.0, 0.05, 0.2, 0.5)[r // 36 % 4]
+            shift = [amp * (2 * rnd() - 1) if abs(fin[i] - at) < wide and rnd() < few else 0.0 for i in range(n)]
+            x = forward(sgs(dur, queue, succ, pred, [fin[i] + lat[i] + shift[i] for i in range(n)])[1])
+        if x[0] <= cur[0] - (0.08 * (1 - r / ROUNDS) + 0.01) * math.log(rnd() + 1e-9):
+            cur, pairs = x, waits(x)
         if x[0] < best[0]:
             best = x
     return best[1]

import math
from concourse.mybir import AluOpType as O, ActivationFunctionType as AF

NC, CH, BL, STEPS = 256, 64, 128, 4
NB, BW_ = NC // BL, BL // 16
GR = 1 + 2 * BL
WB = BL * 16 + 32
f32, bf, i32, u16, f16 = "float32", "bfloat16", "int32", "uint16", "float16"
SCRATCH = {}
for _dt, _names in ((bf, "X:4096 PM:%d AD:4096 AX:4096 AY:4096 d:256 SM:1024 SM2:256 QB:256 W1:1 ON:256 G8:32 G2:8 GN:8 F:144 F0:144 NF:144 F8:144 "
                     "P23:128 N23:128 KW:272 I16:16 MK:256 FD:144 WF:144 BDa:128 BD:128 NBD:128 ID:128 NI:128 N8:128 HI:128 QI:128 SH:128 P4:128 N4:128 R15:128 ETb:2048 BW0:24 F1:144 TR:512 "
                     "TT0:128 TT1:256 OLD:256 NX:256 EQ:256 SC1:256 SC2:512 GE:256 MG:256 XS:256 DS:256 XL:512 AB:512 SG1:256 NA:512 INJ:128 JK:128" % (NB * WB)),
                    (f32, "L:1024 L2:3072 Z2:1536 COL:16 IO:256 CI:64 B32:32 NR:512 CF:32 A1:16 V2:16 RT:128 ZD:256 ZE:512 EZ:256 AC:1 TF:6"),
                    (i32, "D:4112 DO:1024 DI:1024 LI:1024 LJ:1024 EI:256 TH:2 TI:4 PI:2 UI:16 U:16 V3:16 NL:48 N2:32"),
                    (u16, "NU:16 LU:32 LS:16 PU:512 CU:64 C2:48 DU:32 OF:16 OE:32 GL:16"),
                    (f16, "LG:256 SG:256 NH:32 PH:512")):
    for _x in _names.split():
        SCRATCH[_x.split(":")[0]] = ("sbuf", [128, int(_x.split(":")[1])], _dt)
SCRATCH["G"] = ("sbuf", [128, NB * GR * 16], bf)
NK = 4
for _p in ("psU", "psE", "psB0", "psB1"):
    SCRATCH[_p] = ("psum", [128, 512], f32)
for _p in range(NK):
    SCRATCH["psZ%d" % _p] = ("psum", [128, 2048 // NK], f32)
SEMAPHORES = ["cv", "cs", "ct", "cg"] + ["dma%d" % k for k in range(24)] + ["%s%d" % (x, k) for x in ("ls", "rs") for k in range(17)]

CY, PEC, GA, SC, FX, WAKE, HOP, RISS = 0.00095, 0.0005, 1.5, 3.5, 0.05, 0.065, 1.5, 0.5
DL, PL, SX, PX = 2.2, 1.2, 0.06, 0.005
CX, CD = (32, 32), (64, 64)
FORM = ("s", "s")
YS = ((), ())
RX, RQ, MS, PUSH = "v", "v", (False, False), "all"
SPLIT, BK1, BK2 = True, "psZ3", (("psZ0", "psZ1", "psZ2", "psZ3"),) * 2
CUT, STAG, EARLY, ROUNDS, SEED, ORDER = 2048, 4.0, 0.0, 20000, 1, []


def program(g, core, T, topo):
    rank, ops, acc = T.rank_of(core), [], {}
    nsem, bias = [0, 0], [0.0]

    def c(name, lo=0, hi=None, st=1):
        hi = SCRATCH[name][1][-1] if hi is None else hi
        return [(T[name][:, lo:hi:st] if st > 1 else T[name][:, lo:hi], name, lo, hi, st == 1, (hi - lo + st - 1) // st)]

    def gv(r0, r1, k=0, st=1):
        return c("G", 16 * r0 + k, 16 * r1, st)

    def raw(ap, name, lo, hi, full=False):
        return [(ap, name, lo, hi, full, hi - lo)]

    def ind(win, off):
        return [(win[0][0].indirect(off[0][0]),) + win[0][1:5] + (16 * off[0][5],)] + off

    def add(q, dur, outs, ins, call, sem=None, n=1, deps=(), lat=0.0, after=()):
        me, hard, soft = len(ops), set(deps), set(after)
        ops.append({"q": q, "sem": sem})
        both = [(False, x) for x in ins if x[1] is not None] + [(True, x) for x in outs if x[1] is not None]
        for is_w, (_, name, lo, hi, full, _n) in both:
            if name[:2] == "ps":
                e = acc.setdefault(name, [q, [], []])
                if e[0] != q:
                    e[0], e[1], e[2] = q, [], e[1]
                hard.update(e[2])
                e[1].append(me)
                continue
            for (l2, h2, w2, o) in acc.get(name, ()):
                if o != me and l2 < hi and lo < h2 and (is_w or w2):
                    hard.add(o)
        for is_w, (_, name, lo, hi, full, _n) in both:
            if name[:2] != "ps":
                old = acc.get(name, [])
                if is_w and full:
                    old = [a for a in old if not (lo <= a[0] and a[1] <= hi)]
                acc[name] = old + [(lo, hi, is_w, me)]
        soft -= hard
        ops[me] = {"q": q, "dur": dur, "hard": sorted(hard), "soft": sorted(soft), "call": call, "sem": sem, "n": n, "lat": lat, "bias": bias[0]}
        return me

    def cost(out, a, k):
        if len(out) > 1:
            return FX + a[0][5] * SC * CY
        if a is not None and len(a) > 1:
            return FX + a[0][5] * GA * CY
        return FX + max(64, out[0][5] * k) * CY

    def vcopy(out, a, k=1.0):
        return add("v", cost(out, a, k), out[:1], a + out[1:], lambda: g.vector.tensor_copy(out=out[0][0], in_=a[0][0]))

    def vtt(out, a, b, op):
        ps = a[0][1][:2] == "ps" or b[0][1][:2] == "ps"
        return add("v", cost(out, a, 1.0 if ps else 2.0), out[:1], a + b + out[1:],
                   lambda: g.vector.tensor_tensor(out=out[0][0], in0=a[0][0], in1=b[0][0], op=op))

    def vts(out, a, s1, s2, o0, o1=None, k=1.0):
        ex = [x for s in (s1, s2) if isinstance(s, list) for x in s]
        v1, v2 = [s[0][0] if isinstance(s, list) else s for s in (s1, s2)]
        kw = {"op0": o0} if o1 is None else {"op0": o0, "op1": o1}
        return add("v", cost(out, a, k), out, a + ex,
                   lambda: g.vector.tensor_scalar(out=out[0][0], in0=a[0][0], scalar1=v1, scalar2=v2, **kw))

    def vset(out, v, k=1.0):
        return add("v", cost(out, None, k), out, [], lambda: g.vector.memset(out[0][0], v))

    def scan(out, a, mask, k):
        return add("v", cost(out, None, k), out, a + mask, lambda: g.vector.tensor_tensor_scan(
            out=out[0][0], data0=a[0][0], data1=mask[0][0], initial=0.0, op0=O.max, op1=O.mult))

    def act(out, a, fn, bias=None, scale=None, accum=None):
        kw = {}
        if bias is not None:
            kw["bias"] = bias[0][0] if isinstance(bias, list) else bias
        if scale is not None:
            kw["scale"] = scale[0][0] if isinstance(scale, list) else scale
        if accum is not None:
            kw["accum_out"] = accum[0][0]
        return add("s", cost(out, a, 1.0) + (SX if len(a) == 1 else 0.01), out + (accum or []), a + [x for s in (bias, scale) if isinstance(s, list) for x in s],
                   lambda: g.scalar.activation(out=out[0][0], in_=a[0][0], func=fn, **kw))

    def mm(lst, after=()):
        def call():
            x = None
            for (o, l, r, s, e) in lst:
                x = g.tensor.matmul(out=o[0][0], lhsT=l[0][0], rhs=r[0][0], start=s, stop=e)
            return x
        return add("t", PX + sum(max(64, x[2][0][5]) for x in lst) * PEC, [lst[0][0][0]], [v for x in lst for v in x[1] + x[2]], call, after=after, lat=0.03)

    def grp(parts, lst, last=False):
        if lst:
            parts.append(mm([x + (not parts and n == 0, last and n == len(lst) - 1) for n, x in enumerate(lst)], after=parts if last else parts[:1]))

    def one(lst):
        grp([], lst, True)

    def dma(q, out, a, us, calls=None):
        s = "dma%d" % nsem[0]
        nsem[0] += 1
        lst = calls or [(out[0][0], a[0][0])]

        def call():
            for (o, i) in lst:
                {"y": g.sync, "s": g.scalar}[q].dma_start(o, i).then_inc(T.sem[s], 16)
        return add(q, 0.1 * len(lst), out, a, call, sem=s, n=16 * len(lst), lat=us)

    def send(to, src, dst, us=0.0):
        to = T.cores[to]
        if not topo.may_write(core, to):
            raise ValueError("this core may not write to core %d" % to)
        eng = topo.engines(core, to)
        mask = sum(1 << e for e in eng)
        rid, pid = topo.addr(to)[:2]
        ls, rs = "ls%d" % nsem[1], "rs%d" % nsem[1]
        nsem[1] += 1

        def call():
            g.remote_dma(dst[0][0], src[0][0], T.sem[rs], T.sem[ls], pid, rid, mask)
        o = add("g", RISS, [], src, call, sem=ls, n=len(eng), lat=HOP + us - RISS)
        add(rs, 0.0, dst, [], None, sem=rs, n=len(eng), deps=(o,))
        return o

    def reader(t):
        return (rank - 1 - t % 3) % 4

    def dram(ap):
        return [(ap, None, 0, 0, False, 0)]

    def asel(out, a, pat, op, base, cm, deps=()):
        return add("g", 0.2 + out[0][5] * 2 * CY, out, a, lambda: g.affine_select(
            out=out[0][0], in_=a[0][0], pattern=pat, compare_op=op, fill=0.0, base=base, channel_multiplier=cm), deps=deps)

    def iota(out, pat, base, cm):
        return add("g", 0.15 + out[0][5] * 2 * CY, out, [], lambda: g.iota(
            out[0][0], pat, base, cm, allow_small_or_imprecise_dtypes=True))

    bias[0] = 100.0
    dma("y", c("QB"), dram(T.qd[:, :]), 2.0)
    dma("s", c("W1"), dram(T.wt[:]), 2.0)
    bias[0] = 200.0
    vset(c("ON"), 1.0, 0.5)
    vset(c("F"), 0.0, 0.5)
    asel(c("G8", 0, 8), c("ON", 0, 8), [[-16, 8]], O.is_ge, 0, 1)
    asel(c("G8", 8, 16), c("G8", 0, 8), [[16, 8]], O.is_ge, 15, -1)
    G1 = c("G8", 8, 16)
    bias[0] = 100.0
    DROW = [raw(T.D[j:128:16, 0:4096], "D", 0, 4096) for j in range(2)]
    dma("y", c("DO", 0, 256), dram(T.dr[:, :]), 2.2)
    dma("s", c("LI"), dram(T.lg[:, :]), 3.0)
    send(reader(0), c("DO", 0, 256), c("DI", 0, 256), 2.0)
    so = send(reader(0), c("LI"), c("LJ"), 3.0)
    vcopy(c("F", 16, 144, 16), G1)
    vts(c("WF"), c("F"), c("W1"), None, O.mult)
    iota(c("PI", 0, 1), [[0, 1]], 0, 1)
    iota(c("CI", 48, 64), [[1, 16]], 0, 0)
    bias[0] = 0.0
    for k in range(2):
        dma("ys"[k], c("X", 2048 * k, 2048 * k + 2048), dram(T.xr[:, 2048 * k:2048 * k + 2048]), 4.0)
    dma("s", c("EI"), dram(T.e0[:, :]), 4.0)
    dma("y", raw(T.TH[:, :], "TH", 0, 2, True), dram(None), 4.0, [(T.TH[j:128:16, :], T.th[:, :]) for j in range(16)])
    for k in range(0, CUT, 512):
        vset(c("D", k, k + 512), 0.0)
    for k in range(CUT, 4112, 520):
        iota(c("D", k, min(k + 520, 4112)), [[0, min(520, 4112 - k)]], 0, 0)
    dma("y", DROW[0], dram(T.dr[:, :]), 2.5)
    asel(c("F0"), c("F"), [[-1, 144]], O.is_equal, 16, 1)
    asel(c("F1"), c("F"), [[-1, 144]], O.is_equal, 15, 1)
    iota(c("CI", 0, 16), [[0, NB], [64, BW_]], 0, 0)
    iota(c("CI", 16, 32), [[256, 16]], 0, 0)
    iota(c("CI", 32, 48), [[0, 2], [256, BW_]], 2048, 0)
    iota(c("IO"), [[0, 16], [1, 16]], 0, 0)
    iota(c("TR", 256, 512), [[4, 256]], 0, 0)
    vts(c("PI", 1, 2), c("PI", 0, 1), 15, None, O.bitwise_and)
    K = c("COL", 0, 1)
    vcopy(K, c("PI", 1, 2))
    act(c("COL", 1, 2), K, AF.Copy, scale=16.0)
    act(c("COL", 2, 3), K, AF.Copy, scale=4.0)
    act(c("COL", 3, 4), K, AF.Identity, bias=2048.0)
    vts(c("COL", 4, 5), K, 15.0, None, O.is_equal)
    for j, v in enumerate((-16.0, -1.0, -12288.0)):
        vts(c("COL", 5 + j, 6 + j), K, float(j), v, O.is_equal, O.mult)
    K15 = c("COL", 4, 5)
    act(c("B32", 0, 16), c("CI", 0, 16), AF.Identity, bias=c("COL", 2, 3))
    act(c("B32", 16, 32), c("CI", 16, 32), AF.Identity, bias=c("COL", 1, 2))
    act(c("BW0", 0, 8), c("CI", 16, 24), AF.Identity, bias=c("COL", 1, 2))
    act(c("KW", 256, 272), c("CI", 32, 48), AF.Identity, bias=c("COL", 1, 2))
    vcopy(c("GL"), c("CI", 48, 64))
    vts(c("I16"), c("CI", 48, 64), K, None, O.is_equal)
    vts(c("TR", 0, 256), c("IO"), K, 8192.0, O.is_le, O.mult)
    asel(c("BDa"), c("ON", 0, 128), [[-16, 8], [0, 16]], O.is_ge, 0, 1)
    asel(c("BD"), c("BDa"), [[16, 8], [0, 16]], O.is_ge, 15, -1)
    asel(c("ID"), c("ON", 0, 128), [[-1, 128]], O.is_equal, 0, 1)
    asel(c("BDa"), c("BD"), [[1, 128]], O.is_equal, -1, -1)
    for k in range(8):
        asel(c("ETb", 256 * k, 256 * k + 256), c("ON"), [[-1, 2], [-16, 8], [0, 16]], O.is_equal, -2 * k, 1, deps=(so,))
    act(c("COL", 8, 9), K15, AF.Copy, scale=16.0)
    act(c("COL", 10, 11), c("COL", 5, 6), AF.Identity, scale=2049.0 / 131072, bias=1.0 / 8192)
    asel(c("INJ"), c("BD"), [[1, 128]], O.is_equal, 15, -1)
    for nm, src, v in (("NI", "ID", -1.0), ("N8", "ID", -8192.0), ("HI", "ID", 0.5), ("QI", "ID", -0.25), ("P4", "ID", 4096.0), ("N4", "ID", -4096.0),
                       ("NBD", "BD", -1.0), ("SH", "BDa", 8192.0), ("NF", "F", -1.0), ("F8", "F", 8192.0),
                       ("FD", "F", c("COL", 10, 11))) + ((("P23", "ID", 8388608.0), ("N23", "ID", -8388608.0)) if "t" in RX + RQ else ()):
        act(c(nm), c(src), AF.Copy, scale=v)
    act(c("G2"), G1, AF.Copy, scale=2.0)
    act(c("GN"), G1, AF.Copy, scale=-1.0)
    act(c("R15"), c("ON", 0, 128), AF.Copy, scale=c("COL", 8, 9))
    act(c("KW", 0, 256), c("ON"), AF.Copy, scale=-10240.0)
    for k in range(4):
        asel(c("SM", 256 * k, 256 * k + 256), c("ON"), [[0, 16], [1, 16]], O.not_equal, -15, 0, deps=(so,))
    asel(c("SM2"), c("ON"), [[0, 8], [1, 32]], O.not_equal, -1, 0, deps=(so,))
    for b in range(NB):
        act(c("PM", b * WB + 16, b * WB + 32), c("ON", 0, 16), AF.Copy, scale=0.0)
        act(gv(b * GR, b * GR + 1), c("ON", 0, 16), AF.Copy, scale=0.0)
    asel(c("L"), c("LI"), [[0, 1024]], O.is_ge, 0, 0, deps=(so,))
    vts(c("TI", 0, 2), c("TH"), 4, None, O.arith_shift_right)
    vts(c("TI", 2, 4), c("TH"), 15, None, O.bitwise_and)
    vts(c("TF", 0, 2), c("TI", 0, 2), c("COL", 5, 6), None, O.mult)
    vts(c("TF", 2, 4), c("TI", 2, 4), 0.5, c("COL", 6, 7), O.add, O.mult)
    vtt(c("TF", 4, 6), c("TF", 0, 2), c("TF", 2, 4), O.add)
    vtt(c("TF", 0, 1), c("TF", 5, 6), c("COL", 7, 8), O.add)
    act(c("TT0"), c("BD"), AF.Copy, scale=c("TF", 4, 5))
    for j in range(2):
        act(c("TT1", j, 256, 2), c("BD"), AF.Copy, scale=c("TF", 0, 1))
    ONE = c("ON", 0, 128)

    def sel(name, m):
        return c(name, 16 - m, 144 - m)

    def wrap(out, name, v, lo, hi):
        return [(out, sel(name, m), c(v, lo + m, hi, 16)) for m in range(16)]

    def half(out, ps, terms, how):
        one([(ps, c("QI"), ONE)] + [(ps, c("HI"), x) for x in terms] + ([(ps, c("P23"), ONE), (ps, c("N23"), ONE)] if how == "t" else []))

        def rest():
            if how == "v":
                vts(out, ps, 8388608.0, 8388608.0, O.add, O.subtract)
            elif how == "t":
                act(out, ps, AF.Copy)
            else:
                act(c("RT"), ps, AF.Identity, bias=8388608.0)
                act(out, c("RT"), AF.Identity, bias=-8388608.0)
        return rest

    rot = [0]

    def bank(names):
        rot[0] += 1
        return names[rot[0] % len(names)]

    for t in range(STEPS):
        to, last = reader(t + 1), t == STEPS - 1
        cu, cv = 32 * (t % 2), 32 * ((t + 1) % 2)
        LT, L2 = (c("L"), c("L2", 1024 * (t - 1), 1024 * t)) if t else (c("LI"), c("LJ"))
        if not last and PUSH == "new":
            send(to, c("L"), c("L2", 1024 * t, 1024 * t + 1024), 3.0)
        N = c("NL", 0, 16)
        for i0, i1, W, W2 in ((0, BL, "psU", "psU"), (BL, NC, "psE", "psE")) if t and SPLIT else ((0, NC, "psU", "psE"),):
            w0, w1 = i0 // 16, i1 // 16
            UI, U, A1, V2, V3, NL, NU, LU, LS = [c(x, w0, w1) for x in ("UI", "U", "A1", "V2", "V3", "NL", "NU", "LU", "LS")]
            bias[0] = STAG * (i0 == 0)
            one(wrap(c(W, w0, w1), "WF", "QB", i0, i1))
            vcopy(UI, c(W, w0, w1))
            vts(U, UI, 4095, None, O.bitwise_and)
            vts(A1, U, 592.0, None, O.add)
            vtt(V2, A1, A1, O.mult)
            if t:
                vts(V3, V2, c("AC"), 75520.0, O.add, O.add)
            else:
                vts(V3, V2, 42752.0, None, O.add)
            vts(NL, V3, 5, 4095, O.arith_shift_right, O.bitwise_and)
            if t:
                vcopy(NU, NL)
            if t:
                vcopy(c("LG", i0, i1), ind(c("D", 0, 4096), NU))
            else:
                vts(c("N2", 0, 16), NL, 8, None, O.arith_shift_right)
                vts(c("N2", 16, 32), NL, 255, None, O.bitwise_and)
                vcopy(c("DU"), c("N2"))
                act(c("MK"), ind(c("I16"), c("DU", 0, 16)), AF.Copy)
                vtt(c("LG"), ind(c("DO", 0, 256), c("DU", 16, 32)), c("MK"), O.mult)
                vtt(c("SG"), ind(c("DI", 0, 256), c("DU", 16, 32)), c("MK"), O.mult)
            if t and SPLIT:
                LU, LS = c("LU", 2 * w0, 2 * w0 + BW_), c("LU", 2 * w0 + BW_, 2 * w1)
                one(wrap(c(W, 32, 40), "F0", "LG", i0, i1))
                one(wrap(c(W, 40, 48), "F1", "LG", i0, i1))
                vcopy(c("LU", 2 * w0, 2 * w1), c(W, 32, 48))
                vcopy(c("PU", i0, i1), ind(LT, LU))
                vcopy(c("PU", NC + i0, NC + i1), ind(L2, LS))
                continue
            one(wrap(c(W, 32 + w0, 32 + w1), "F0" if t else "F", "LG", i0, i1))
            vcopy(LU, c(W, 32 + w0, 32 + w1))
            vcopy(c("PU", i0, i1), ind(LT, LU))
            one(wrap(c(W2, w0, w1), "F1" if t else "F", "LG" if t else "SG", i0, i1))
            vcopy(LS, c(W2, w0, w1))
            vcopy(c("PU", NC + i0, NC + i1), ind(L2, LS))
        bias[0] = 0.0
        for a in range(0, NC, CH):
            r0 = a // BL * GR + 1 + a % BL
            for h in range(0, CH, CX[a // BL]):
                act(gv(r0 + h, r0 + h + CX[a // BL]), ind(c("X"), c("PU", a + h, a + h + CX[a // BL])), AF.Copy)
            y0 = a // BL * WB + 17 + 16 * (a % BL)
            scan(c("PM", y0, y0 + 16 * CH), gv(r0, r0 + CH), c("SM", 0, 16 * CH), 0.5)
        vts(c("PH"), c("PU"), -2048.0, None, O.add, k=0.5)
        vts(c("NL", 16, 32), c("UI"), 3, None, O.bitwise_and)
        vts(c("NL", 32, 48), c("UI"), 15, None, O.bitwise_and)
        vtt(c("CF"), c("NL", 16, 48), c("B32"), O.add)
        vcopy(c("CU", cu, cu + 32), c("CF"))
        act(c("OLD"), ind(c("X"), c("CU", cu + 16, cu + 32)), AF.Copy)
        if not last:
            bias[0] = EARLY
            if PUSH == "new":
                send(to, c("CU", cu, cu + 16), c("C2", 16 * t, 16 * t + 16))
            vts(c("NH"), c("NL", 0, 32), -2048.0, None, O.add)
            one([(c(BK1, 0, 512), c("ID"), c("TR"))] + [(c(BK1, m, 512, 16), c("ETb", 128 * m, 128 * m + 128), c("NH")) for m in range(16)])
            act(c("NR"), c(BK1, 0, 512), AF.Identity, bias=2048.0)
            vtt(c("EQ"), ind(N, c("GL")), c("NR", 0, 256), O.is_equal)
            one([(c(BK1, 0, 16), c("ID"), c("NH", 0, 16))] + wrap(c(BK1, 0, 16), "F8", "EQ", 0, NC))
            vts(c("DU", 0, 32, 2), c(BK1, 0, 16), c("COL", 3, 4), 2048.0, O.min, O.add)
            for n in range(15, -1, -1):
                vcopy(ind(c("D"), c("DU", 2 * n, 2 * n + 1)), c("NR", 256 + 16 * n, 272 + 16 * n))
            DO, DI = [c(x, 256 * t + 256, 256 * t + 512) for x in ("DO", "DI")]
            dma("y", DO, DROW[0], DL)
            send(to, DO, DI, DL - 1.5)
            dma("y", DROW[1], DI, DL)
        for b in range(NB):
            i0, i1, w0, w1, x0 = b * BL, (b + 1) * BL, b * BW_, (b + 1) * BW_, b * GR + 1
            y0, B = x0 + BL, ("psU", "psE")[b]
            bias[0] = STAG * (NB - 1 - b)
            part = []
            grp(part, [(c(B, 0, 128), ONE, c("TT0"))])
            for a in range(0, BL, CH):
                for h in range(a, a + CH, CD[b]):
                    names = ind(c("X"), c("PU", NC + i0 + h, NC + i0 + h + CD[b]))
                    vtt(gv(y0 + h, y0 + h + CD[b]), names, gv(x0 + h, x0 + h + CD[b]), O.subtract)
                if FORM[b] == "s":
                    act(c("AD", 16 * (i0 + a), 16 * (i0 + a + CH)), gv(y0 + a, y0 + a + CH), AF.Abs)
                else:
                    vts(c("AD", 16 * (i0 + a), 16 * (i0 + a + CH)), gv(y0 + a, y0 + a + CH), 0.0, None, O.max, k=0.5)
            if FORM[b] == "v":
                grp(part, [(c(B, k, 128, 16), gv(y0, y0 + BL, k, 16), c("GN")) for k in range(15)])
            grp(part, [(c(B, k, 128, 16), c("AD", 16 * i0 + k, 16 * i1, 16), G1 if FORM[b] == "s" else c("G2")) for k in range(15)], True)
            GE = c("GE", i0, i1)
            scan(c("SC1", i0, i1), c(B, 0, 128), c("SM", 0, 128), 1.0)
            one([(c(B, 128, 256), c("SC1", i0, i1), c("ID"))])
            act(GE, c(B, 128, 256), AF.Sign, bias=K15)
            one([(c(B, 0, BW_), c("ID"), c("BW0", 0, BW_))] + wrap(c(B, 0, BW_), "NF", "GE", i0, i1))
            OF = c("OF", w0, w1)
            vts(OF, c(B, 0, BW_), 16.0, None, O.add)
            M = ind(c("PM", b * WB + 16, b * WB + 16 + 16 * BL), OF)
            if MS[b]:
                act(c("MG", i0, i1), M, AF.Copy)
                one([(c(B, 0, BL), c("NI"), c("QB", i0, i1)), (c(B, 0, BL), c("ID"), c("MG", i0, i1))])
                act(c("d", i0, i1), c(B, 0, BL), AF.Abs)
            else:
                vtt(c("MG", i0, i1), M, c("QB", i0, i1), O.subtract)
                act(c("d", i0, i1), c("MG", i0, i1), AF.Abs)
        for b in range(NB):
            i0, i1, w0, w1, x0 = b * BL, (b + 1) * BL, b * BW_, (b + 1) * BW_, b * GR + 1
            y0, B, W = x0 + BL, "psB%d" % b, ("psU", "psE")[b]
            bias[0] = STAG * (NB - 1 - b)
            d, xs, ds, sg, GE, OF, NA = [c(x, i0, i1) for x in ("d", "XS", "DS", "SG1", "GE")] + [c("OF", w0, w1), c("NA", 2 * i0, 2 * i0 + BL)]
            act(xs, ind(gv(x0, x0 + BL), OF), AF.Copy)
            act(ds, ind(gv(y0, y0 + BL), OF), AF.Copy)
            px, py, pl = c(W, 0, BL), c(W, BL, 2 * BL), c(W, 2 * BL, 3 * BL)
            one([(px, c("ID"), xs), (px, c("NI"), d)])
            one([(py, c("ID"), ds), (py, c("NI"), d), (py, c("ID"), xs)])
            nx = half(c("NX", i0, i1), c(W, 3 * BL, 4 * BL), [c("OLD", i0, i1), d], RX)
            act(c("AB", 2 * i0, 2 * i1), c(W, 0, 2 * BL), AF.Abs)
            if RX != "v":
                nx()
            one([(pl, c("NBD"), c("AB", 2 * i0, 2 * i0 + BL)), (pl, c("N8"), GE), (pl, c("BD"), c("AB", 2 * i0 + BL, 2 * i1))])
            act(sg, pl, AF.Sign, bias=-8192.5, scale=-1.0)
            if b == NB - 1 and not last:
                one([(pl, c("R15"), c("SG1", a, a + BL)) for a in range(0, NC, BL)])
                act(c("JK"), pl, AF.Copy, accum=c("AC"))
            if RX == "v":
                nx()
            vcopy(ind(c("X"), c("CU", cu + 16 + w0, cu + 16 + w1)), c("NX", i0, i1))
            part, ox, oy = [], c(B, 256, 512, 2), c(B, 257, 512, 2)
            grp(part, [(c(B, 256, 512), ONE, c("TT1"))])
            grp(part, [(ox, GE, c("SH")), (oy, GE, c("SH"))])
            ks = [k for k in range(1, 16) if k % NK not in YS[b]]
            for r0, S in ((x0, G1), (y0, c("GN"))):
                grp(part, [(c(B, 257 + 2 * k, 512, 32), gv(r0, r0 + BL, k, 16), S) for k in ks])
            grp(part, [(c(B, 257 + 2 * k0, 512, 2 * NK), d, c("NBD", k0, 128, NK)) for k0 in range(NK) if k0 not in YS[b]] if YS[b] else [(oy, d, c("NBD"))])
            KS, CB = 16 // NK, 32 * NK
            for k0 in range(NK):
                Z, a, dif = bank(BK2[b]), 16 * i0 + KS * BL * k0, [[] for _ in range(0, BL, CB)]
                for h in range(0, BL, CB):
                    grp(dif[h // CB], [(c(Z, KS * h, KS * h + 512), c("NI"), gv(x0 + h, x0 + h + CB, k0, NK))])
                for h in range(0, BL, CB):
                    grp(dif[h // CB], [(c(Z, KS * h + j, KS * h + 512, KS), c("ID"), c("d", i0 + h, i0 + h + CB)) for j in range(KS)], k0 not in YS[b])
                act(c("AX", a, a + KS * BL), c(Z), AF.Abs)
                if k0 in YS[b]:
                    for h in range(0, BL, CB):
                        grp(dif[h // CB], [(c(Z, KS * h, KS * h + 512), c("NI"), gv(y0 + h, y0 + h + CB, k0, NK))], True)
                    act(c("AY", a, a + KS * BL), c(Z), AF.Abs)
                else:
                    vtt(c("AY", a, a + KS * BL), gv(y0, y0 + BL, k0, NK), c(Z), O.max)
                for j, (A, S) in enumerate((("AX", G1), ("AY", G1 if k0 in YS[b] else c("G2")))):
                    grp(part, [(c(B, 256 + 2 * (k0 + NK * h) + j, 512, 32), c(A, a + h, a + KS * BL, KS), S) for h in range(KS) if k0 + h])
            grp(part, [(ox, sg, c("N4")), (oy, sg, c("P4"))], True)
            scan(c("SC2", 2 * i0, 2 * i1), c(B, 256, 512), c("SM2"), 1.0)
            sc = c("SC2", 2 * i0 + 1, 2 * i1, 2)
            one([(c(B, 0, 128), sc, c("ID"))])
            one([(c(B, 128, 256), c("INJ"), sg), (c(B, 128, 256), sc, c("ID"))])
            act(c("NA", 2 * i0, 2 * i1), c(B, 0, 256), AF.Relu, scale=-16384.0, bias=8192.0)
            ZN, EM = c("ZE", 2 * i0, 2 * i0 + BL), c("ZE", 2 * i0 + BL, 2 * i1)
            oe, OE, part = c(B, 2 * BL, 2 * BL + 2 * BW_), c("OE", 2 * w0, 2 * w1), []
            grp(part, [(c(W, 0, 2 * BL), c("ID"), c("KW", 0, 256)), (px, c("ID"), c("PH", i0, i1)), (px, c("N4"), sg),
                       (py, c("ID"), c("PH", NC + i0, NC + i1)), (py, c("P4"), sg)])
            grp(part, [(px, c("ID"), NA), (py, c("ID"), NA)], True)
            one([(oe, c("ID"), c("KW", 256, 272))] + wrap(oe, "FD", "NA", 2 * i0, 2 * i1))
            vts(OE, oe, 16.0, None, O.add)
            act(c("ZD", i0, i1), px, AF.Copy)
            vtt(ZN, py, c("ZD", i0, i1), O.max)
            act(c("XL", 2 * i0, 2 * i1), ind(gv(x0 - 1, y0 + BL), OE), AF.Copy)
            half(c("QB", i0, i1), pl, [d] + [c("XL", a, a + BL) for a in (2 * i0, 2 * i0 + BL)], RQ)()
            LB = c("L", 4 * i0, 4 * i1)
            vtt(EM, ind(LB, c("CU", cv + w0, cv + w1)) if t else c("EI", i0, i1), NA, O.subtract)
            if not last and PUSH == "new":
                z0 = 512 * t + 2 * i0
                send(to, c("ZE", 2 * i0, 2 * i1), c("Z2", z0, z0 + 2 * BL), 0.8)
            vtt(ind(LB, c("CU", cu + w0, cu + w1)), ZN, EM, O.max)
            if last:
                dma("y", dram(T.yl[:, 4 * i0:4 * i1]), LB, 3.0)
            elif PUSH == "new":
                vtt(ind(c("L2", 1024 * t + 4 * i0, 1024 * t + 4 * i1), c("C2", 16 * t + w0, 16 * t + w1)),
                    c("Z2", z0, z0 + BL), c("Z2", z0 + BL, z0 + 2 * BL), O.max)
            else:
                send(to, LB, c("L2", 1024 * t + 4 * i0, 1024 * t + 4 * i1), PL)
        bias[0] = 0.0
        if last:
            dma("y", dram(T.yx[:, :]), c("X"), 4.0)
    dma("s", dram(T.yq[:, :]), c("QB"), 2.0)
    return ops


def sgs(dur, queue, pred, succ, pri):
    n = len(dur)
    left, at, fin, gaps, placed = [len(p) for p in pred], [0.0] * n, [0.0] * n, {q: [(0.0, 1e9)] for q in set(queue)}, []
    ready = [(pri[i], -i) for i in range(n) if not left[i]]
    while ready:
        x = max(ready)
        ready.remove(x)
        i = -x[1]
        free, s, d = gaps[queue[i]], at[i], dur[i]
        j = len(free) - 1
        while j and free[j - 1][1] > s:
            j -= 1
        a, b = free[j]
        while b - (a if a > s else s) < d:
            j += 1
            a, b = free[j]
        if a > s:
            s = a
        f = fin[i] = s + d
        placed.append((s, len(placed), i))
        if s - a > 0.02:
            free[j:j + 1] = [(a, s), (f, b)] if b - f > 0.02 else [(a, s)]
        elif b - f > 0.02:
            free[j] = (f, b)
        else:
            del free[j]
        for k, w in succ[i]:
            left[k] -= 1
            if at[k] < f + w:
                at[k] = f + w
            if not left[k]:
                ready.append((pri[k], -k))
    placed.sort()
    return [x[2] for x in placed], fin


def schedule(ops):
    n = len(ops)
    dur, queue = [o["dur"] for o in ops], [o["q"] for o in ops]
    pred, succ, pri = [[] for _ in ops], [[] for _ in ops], [0.0] * n
    for i, o in enumerate(ops):
        for d in o["hard"] + o["soft"]:
            w = 0.0 if d in o["soft"] else ops[d]["lat"] + WAKE
            pred[i].append((d, w))
            succ[d].append((i, w))
    for i in range(n - 1, -1, -1):
        pri[i] = dur[i] + max([pri[k] + w for k, w in succ[i]] or [ops[i]["lat"]])
    lat, seed = [o["lat"] for o in ops], [SEED]

    def rnd():
        seed[0] = (seed[0] * 1103515245 + 12345) % 2147483648
        return seed[0] / 2147483648

    def forward(p):
        order, fin = sgs(dur, queue, pred, succ, p)
        return max(fin[i] + lat[i] for i in range(n)), order, fin
    def waits(x):
        fin, before, tail, out = x[2], [-1] * n, {}, []
        for i in x[1]:
            before[i] = tail.get(queue[i], -1)
            tail[queue[i]] = i
        i = max(range(n), key=lambda j: fin[j] + lat[j])
        while True:
            s = fin[i] - dur[i]
            k = max([p for p, w in pred[i] if fin[p] + w > s - 1e-6] or [-1])
            if k < 0:
                k = before[i]
                if k < 0 or fin[k] < s - 0.021:
                    return out
                out.append((k, i))
            i = k
    cur = best = forward([pri[i] + ops[i]["bias"] for i in range(n)])
    pairs = waits(cur)
    for r in range(ROUNDS):
        fin = cur[2]
        if r % 4 and pairs:
            p = [dur[i] - fin[i] for i in range(n)]
            for _ in range(1 + r // 4 % 3):
                (u, v), d = pairs[int(rnd() * len(pairs))], (0.01, 0.3, 1.0, 2.0)[int(rnd() * 4)]
                if rnd() < 0.5:
                    todo, top = [v], p[u] + d
                    while todo:
                        a = todo.pop()
                        if p[a] < top:
                            p[a] = top + 1e-4 * rnd()
                            todo.extend(b for b, w in pred[a])
                else:
                    p[u] = p[v] - d
            x = forward(p)
        else:
            at, wide, amp, few = rnd() * cur[0], (2, 5, 10)[r // 4 % 3], (0.5, 1.7, 4.0)[r // 12 % 3], (0.0, 0.05, 0.2, 0.5)[r // 36 % 4]
            shift = [amp * (2 * rnd() - 1) if abs(fin[i] - at) < wide and rnd() < few else 0.0 for i in range(n)]
            x = forward(sgs(dur, queue, succ, pred, [fin[i] + lat[i] + shift[i] for i in range(n)])[1])
        if x[0] <= cur[0] - (0.08 * (1 - r / ROUNDS) + 0.01) * math.log(rnd() + 1e-9):
            cur, pairs = x, waits(x)
        if x[0] < best[0]:
            best = x
    return best[1]


def emit(g, T, ops, order):
    qs = {"v": (g.vector, "cv"), "s": (g.scalar, "cs"), "t": (g.tensor, "ct"), "g": (g, "cg"), "y": (g.sync, None)}
    cnt, known, snap, mark = {}, {}, {}, {}
    for i in order:
        o = ops[i]
        q, kn = o["q"], known.setdefault(o["q"], {})
        if o["call"] is not None:
            need = {}
            for d in o["hard"]:
                s, v = mark[d]
                if kn.get(s, 0) < v and (s not in need or need[s][0] < v):
                    need[s] = (v, d)
            for s in list(need):
                if any(s2 != s and snap[need[s2][1]].get(s, 0) >= need[s][0] for s2 in need):
                    del need[s]
            for s, (v, d) in sorted(need.items()):
                qs[q][0].wait_ge(T.sem[s], v)
                kn[s] = v
                for s2, v2 in snap[d].items():
                    kn[s2] = max(kn.get(s2, 0), v2)
            r = o["call"]()
        s = o["sem"]
        if s is None:
            s = qs[q][1]
            r.then_inc(T.sem[s], 1)
        cnt[s] = cnt.get(s, 0) + o["n"]
        mark[i] = (s, cnt[s])
        snap[i] = dict(kn) if o["call"] is not None else {}
    for s in sorted(cnt):
        if known.get("g", {}).get(s, 0) < cnt[s]:
            g.wait_ge(T.sem[s], cnt[s])


def rank_program(g, core, T, topo):
    if T.rank_of(core) is None:
        return
    ops = program(g, core, T, topo)
    if not ORDER:
        ORDER.extend(schedule(ops))
    emit(g, T, ops, ORDER)
